import numpy as np
import ml_dtypes


def mxq(x, axis, fmt="e4m3"):
    dtype, down = {"e4m3": (ml_dtypes.float8_e4m3fn, 7), "e5m2": (ml_dtypes.float8_e5m2, 14)}[fmt]
    v = np.moveaxis(np.asarray(x, np.float32).astype(ml_dtypes.bfloat16).astype(np.float64), axis, -1)
    blocks = v.reshape(v.shape[:-1] + (-1, 32))
    amax = np.abs(blocks).max(-1, keepdims=True)
    byte = np.maximum(np.where(amax > 0, np.frexp(amax)[1] - 1 + 127, 0) - down, 1)
    scale = np.exp2(byte - 127.0)
    codes = (blocks / scale).astype(np.float32).astype(dtype).astype(np.float64)
    return np.moveaxis((codes * scale).reshape(v.shape), -1, axis)


WIDE = False


def mx_kscale(k):
    if not WIDE:
        return np.ones(k)
    levels = np.array([10, -10, 5, -5, 0])
    if k % 512:
        return np.exp2(np.random.permutation(np.resize(levels, k // 32))).repeat(32)
    a = np.empty((k // 512, 16))
    for p in range(k // 512):
        a[p, :8] = np.random.permutation(np.resize(levels, 8))
        for g in range(8):
            far = levels[np.abs(levels - a[p, g]) >= 10]
            a[p, g + 8] = far[np.random.randint(len(far))]
    return np.exp2(a.ravel()).repeat(32)


def f64(x):
    return np.asarray(x).astype(np.float64)


def striped(idx):
    return np.tile(idx.reshape(-1, 16).T, (8, 1)).astype(np.uint16)


def unstriped(offs):
    return offs[:16].T.reshape(-1).astype(np.int64)


def striped8(idx):
    return np.concatenate([x.reshape(-1, 16).T for x in idx]).astype(np.uint16)


def runs(offs, k):
    lists = np.stack([offs[16 * r : 16 * r + 16].T.reshape(-1) for r in range(8)]).astype(np.int64)
    return lists[np.arange(k) % 512 // 64]


def pack_weight(w):
    k, n = w.shape
    w = f64(np.asarray(w, np.float32).astype(ml_dtypes.bfloat16)).reshape(k // 32, 32, n)
    amax = np.abs(w).max(1)
    byte = np.clip(np.where(amax > 0, np.frexp(amax)[1] - 1 + 127 - 7, 1), 1, 254)
    scaled = (w * np.exp2(127.0 - byte)[:, None, :]).reshape(k, n).astype(np.float32)
    words = np.ascontiguousarray(scaled.reshape(k // 512, 128, 4, n).transpose(0, 1, 3, 2)).astype(ml_dtypes.float8_e4m3fn).view(np.uint8)
    return words, np.ascontiguousarray(byte.astype(np.uint8).reshape(k // 512, 16, n))


def unpack_weight(words, scales):
    g, p, n, _ = words.shape
    vals = np.ascontiguousarray(words).view(ml_dtypes.float8_e4m3fn).astype(np.float64) * np.repeat(np.exp2(scales.astype(np.float64) - 127.0), 8, axis=1)[..., None]
    return vals.transpose(0, 1, 3, 2).reshape(g * 512, n)


K, T, S, N, H = 512, 2048, 512, 512, 512


def setup_inputs():
    n = np.random.standard_normal
    s = mx_kscale(K)[:, None]
    u = mx_kscale(H)
    packed_xT = pack_weight(n((K, T)) * s)
    return {
        "x_words": packed_xT[0],
        "x_scales": packed_xT[1],
        "w1": (n((K, H)) / np.sqrt(K) / s).astype(np.float32),
        "rec": (0.3 * n((H, S))).astype(np.float32),
        "gn": (np.random.uniform(0.5, 1.5, (H, 1)) * u[:, None]).astype(np.float32),
        "w2": (n((H, N)) / np.sqrt(H) / u[:, None]).astype(np.float32),
        "offs": striped(np.random.permutation(T)[:S]),
        "west": striped8(np.stack([np.random.permutation(S) for _ in range(8)])),
        "east": striped8(np.stack([np.random.permutation(S) for _ in range(8)])),
    }


def reference(x_words, x_scales, w1, rec, gn, w2, offs, west, east):
    xq = unpack_weight(x_words, x_scales)[:, unstriped(offs)]
    y = np.tanh(mxq(f64(w1), 0, "e4m3").T @ xq)
    z = f64(gn) * (1.5 * y - (0.3125 * (y * ((y) ** 2))) - f64(rec) + 0.25 * (y[np.arange(H)[:, None], runs(west, H)] + y[np.arange(H)[:, None], runs(east, H)] - (2.0 * y)))
    return mxq(f64(w2), 0, "e4m3").T @ mxq(z, 0, "e4m3")

@@ -1,0 +1,183 @@
+import math
+from contextlib import ExitStack
+
+import concourse.mybir as mybir
+from concourse.masks import make_identity
+
+F32 = mybir.dt.float32
+BF16 = mybir.dt.bfloat16
+I32 = mybir.dt.int32
+U32 = mybir.dt.uint32
+U16 = mybir.dt.uint16
+U8 = mybir.dt.uint8
+FP8X4 = mybir.dt.float8_e4m3fn_x4
+ALU = mybir.AluOpType
+ACT = mybir.ActivationFunctionType
+
+K, T, S, N, H = 512, 2048, 512, 512, 512
+P = 128
+PACK = 4
+LIST_ROWS = 16
+SUM_BANKS = ((1, 2), (0, 3), (5, 4))
+BACK_BANKS = (6, 7, 3)
+OUT_BANKS = ((1, 2), (0,), (5, 6))
+CHUNKS = (256, 128, 128)
+SIGMOID_PAIR = 1
+FLOPS = 2 * K * H * S + 2 * H * N * S
+
+
+def tile_picked_fhn8_none_p_kernel(tc, x_words, x_scales, w1, rec, gn, w2, offs, west, east, out):
+    nc = tc.nc
+    with ExitStack() as ctx:
+        keep = ctx.enter_context(tc.tile_pool(name="keep", bufs=1))
+        head = ctx.enter_context(tc.tile_pool(name="head", bufs=1))
+        psum = ctx.enter_context(tc.psum_pool(name="psum", bufs=1))
+
+        def bank(number):
+            return psum.tile([P, S], F32, name="bank_%d" % number)
+
+        offs_sb = keep.tile([P, S // LIST_ROWS], U16, name="offs_sb")
+        west_sb = keep.tile([P, S // LIST_ROWS], U16, name="west_sb")
+        east_sb = keep.tile([P, S // LIST_ROWS], U16, name="east_sb")
+        xw_table = head.tile([P, T], U32, name="xw_table", offset=0, align_bytes=64)
+        xs_table = keep.tile([P, T], U8, name="xs_table", tag="xs_then_w1", align_bytes=64)
+        gain = keep.tile([P, PACK], F32, name="gain", tag="w_raw", align_bytes=64)
+
+        nc.vector.memset(xs_table[:].bitcast(I32), 0)
+        nc.sync.dma_start(gain[:], gn.rearrange("(p t) o -> p (t o)", t=PACK))
+        nc.sync.dma_start(offs_sb[:], offs)
+        nc.sync.dma_start(xw_table[:].bitcast(I32), x_words[0].rearrange("p n t -> p (n t)").bitcast(I32))
+        for q in range(4):
+            nc.scalar.dma_start(xs_table[32 * q : 32 * q + 4, :].bitcast(I32), x_scales[0, 4 * q : 4 * q + 4, :].bitcast(I32))
+        nc.sync.dma_start(west_sb[:], west)
+        nc.sync.dma_start(east_sb[:], east)
+
+        ident = keep.tile([P, P], F32, name="ident", align_bytes=64)
+        make_identity(nc, ident[:])
+        warm = keep.tile([P, 1], F32, name="warm")
+        nc.scalar.activation(warm[:], ident[:, 0:1], ACT.Sigmoid)
+
+        x_codes = keep.tile([P, S], U32, name="x_codes", align_bytes=64)
+        nc.vector.tensor_copy(x_codes[:], xw_table[:].indirect(offs_sb[:]))
+        x_scale = head.tile([P, S], U8, name="x_scale", offset=0, align_bytes=64)
+        nc.vector.tensor_copy(x_scale[:], xs_table[:].indirect(offs_sb[:]))
+
+        def transpose_into(dst, src, start, stop):
+            nc.tensor.matmul(dst, lhsT=src, rhs=ident[:], start=start, stop=stop, is_transpose=True)
+
+        weight = [2.0 if t // 2 == SIGMOID_PAIR else 1.0 for t in range(PACK)]
+        gain_bank = bank(0)
+        for t in range(PACK):
+            transpose_into(gain_bank[:, t * P : (t + 1) * P], gain[:, t : t + 1].to_broadcast([P, P]), True, True)
+        w1_raw = keep.tile([P, PACK, H], F32, name="w1_raw", tag="w_raw", align_bytes=64)
+        nc.sync.dma_start(w1_raw[:], w1.rearrange("(p j) c -> p j c", j=PACK))
+        rec_all = head.tile([P, PACK, S], F32, name="rec_all", offset=S, align_bytes=64)
+        rec_rows = rec.rearrange("(p t) s -> p t s", t=PACK)
+        for t in range(PACK):
+            nc.sync.dma_start(rec_all[:, t, :], rec_rows[:, t, :])
+        rec_sb = [rec_all[:, t, :] for t in range(PACK)]
+
+        gain_row = keep.tile([P, 2, 2, P, 2], F32, name="gain_row", align_bytes=64)
+        for t in range(PACK):
+            nc.scalar.activation(gain_row[:, t // 2, :, :, t % 2], gain_bank[:, t * P : (t + 1) * P].unsqueeze(1).to_broadcast([P, 2, P]),
+                                 ACT.Copy, scale=-1.0 / weight[t])
+
+        w1_cols = w1_raw[:].rearrange("p j (m t) -> p m j t", t=PACK)
+        y, ysq, cubic = [], [], []
+        logit = {}
+        for t in range(PACK):
+            if t % 2 == 0:
+                w1_pair = keep.tile([P, 2, P, PACK], BF16, name="w1_pair_%d" % t, tag="xs_then_w1", align_bytes=64)
+                nc.vector.tensor_copy(w1_pair[:].rearrange("p t m j -> p m j t"), w1_cols[:, :, :, t : t + 2])
+            codes = keep.tile([P, P], U32, name="w1_codes_%d" % t, align_bytes=64)
+            scale = keep.tile([P, P], U8, name="w1_scale_%d" % t, align_bytes=64)
+            nc.vector.quantize_mx(out=codes[:].bitcast(FP8X4), scales=scale[:],
+                                  in_=w1_pair[:, t % 2].rearrange("p m j -> p (m j)"))
+            acc = bank(1 + t)
+            nc.tensor.matmul_mx(out=acc[:], lhsT=codes[:].bitcast(FP8X4), lhsT_scale=scale[:],
+                                rhs=x_codes[:].bitcast(FP8X4), rhs_scale=x_scale[:], start=True, stop=True)
+            y.append(keep.tile([P, S], F32, name="y_%d" % t, align_bytes=64))
+            ysq.append(keep.tile([P, S], F32, name="ysq_%d" % t, tag="ysq_%d" % t, align_bytes=64))
+            nc.scalar.activation(y[t][:], acc[:], ACT.Tanh)
+            nc.scalar.activation(ysq[t][:], y[t][:], ACT.Square, scale=math.sqrt(0.3125 * weight[t]))
+            if t // 2 == SIGMOID_PAIR:
+                logit[t] = keep.tile([P, S], F32, name="logit_%d" % t, align_bytes=64)
+                nc.scalar.activation(logit[t][:], acc[:], ACT.Copy, scale=-2.0)
+
+        w2_raw = keep.tile([P, PACK, N], F32, name="w2_raw", tag="w_raw", align_bytes=64)
+        nc.sync.dma_start(w2_raw[:], w2.rearrange("(p j) c -> p j c", j=PACK))
+        w2_codes = keep.tile([P, N], U32, name="w2_codes", align_bytes=64)
+        w2_scale = keep.tile([P, N], U8, name="w2_scale", align_bytes=64)
+
+        def prepare_w2():
+            grouped = keep.tile([P, N, PACK], BF16, name="w2_grouped", align_bytes=64)
+            nc.vector.tensor_copy(grouped[:].rearrange("p (c i) j -> p c j i", i=4), w2_raw[:].rearrange("p j (c i) -> p c j i", i=4))
+            nc.vector.quantize_mx(out=w2_codes[:].bitcast(FP8X4), scales=w2_scale[:], in_=grouped[:].rearrange("p c j -> p (c j)"))
+
+        first = 0
+        for c, width in enumerate(CHUNKS):
+            last = c == len(CHUNKS) - 1
+            blocks = width // P
+            cells = slice(first, first + width)
+            entries = slice(first // LIST_ROWS, (first + width) // LIST_ROWS)
+            if c == 0:
+                tags = ("near_0_0", "ysq_0", "near_0_2", "near_0_3")
+                near = [keep.tile([P, 2, width], F32, name="near_0_%d" % t, tag=tags[t], align_bytes=64)[:] for t in range(PACK)]
+            else:
+                near_low = keep.tile([P, 2, 2, width], F32, name="near_low_%d" % c, tag=(None, "ysq_3", "zt_0_1")[c], align_bytes=64)
+                near_top = keep.tile([P, 2, 2, width], F32, name="near_top_%d" % c, align_bytes=64)
+                near = [near_low[:, 0], near_low[:, 1], near_top[:, 0], near_top[:, 1]]
+            zt = {}
+            for u in ((1, 0) if last else (0, 1)):
+                sums = bank(SUM_BANKS[c][u])
+                early, late = [], []
+                for e in range(2):
+                    t = 2 * u + e
+                    for side, lst in enumerate((west_sb, east_sb)):
+                        if u == SIGMOID_PAIR:
+                            nc.scalar.activation(near[t][:, side, :], logit[t][:].indirect(lst[:, entries]), ACT.Sigmoid)
+                        else:
+                            nc.vector.tensor_scalar(near[t][:, side, :], y[t][:].indirect(lst[:, entries]), -0.25, 0.0, ALU.mult, ALU.add)
+                    if c == 0:
+                        cubic.append(keep.tile([P, S], F32, name="cubic_%d" % t, align_bytes=64))
+                        nc.vector.scalar_tensor_tensor(cubic[t][:], ysq[t][:], weight[t], y[t][:], ALU.subtract, ALU.mult)
+                    places = [(sums[:, (e * blocks + b) * P : (e * blocks + b + 1) * P], slice(b * P, (b + 1) * P),
+                               slice(first + b * P, first + (b + 1) * P)) for b in range(blocks)]
+                    recs = [(dst, rec_sb[t][:, own]) for dst, here, own in places] * int(weight[t])
+                    cubics = [(dst, cubic[t][:, own]) for dst, here, own in places]
+                    gathered = [(dst, near[t][:, side, here]) for side in range(2) for dst, here, own in places]
+                    if c == 0 and u != SIGMOID_PAIR:
+                        early, late = early + recs, late + gathered + cubics
+                    else:
+                        early, late = early + recs + cubics, late + gathered
+                terms = early + late
+                for i, (dst, term) in enumerate(terms):
+                    transpose_into(dst, term, i == 0, i == len(terms) - 1)
+                zt[u] = keep.tile([P, width, 2], BF16, name="zt_%d_%d" % (c, u), tag="zt_%d_%d" % (c, u), align_bytes=64)
+                nc.vector.scalar_tensor_tensor(zt[u][:], sums[:, 0 : 2 * width].rearrange("q (e n) -> q n e", e=2), float(u),
+                                               gain_row[:, u, 0:blocks].rearrange("q b p e -> q (b p) e"), ALU.subtract, ALU.mult)
+            if c == 0:
+                prepare_w2()
+            back = bank(BACK_BANKS[c])
+            for u in zt:
+                for b in range(blocks):
+                    words = zt[u][:, b * P : (b + 1) * P].rearrange("q p e -> q (p e)").bitcast(F32)
+                    transpose_into(back[:, (u * blocks + b) * P : (u * blocks + b + 1) * P], words, True, True)
+            z16 = keep.tile([P, width * PACK], BF16, name="z16_%d" % c, tag="z16_%d" % c, align_bytes=64)
+            unpack = nc.vector.tensor_copy if last else nc.scalar.copy
+            unpack(z16[:].bitcast(F32).rearrange("p (n u) -> p n u", u=2), back[:, 0 : 2 * width].rearrange("p (u n) -> p n u", u=2))
+            z_codes = keep.tile([P, width], U32, name="z_codes_%d" % c, align_bytes=64)
+            z_scale = keep.tile([P, width], U8, name="z_scale_%d" % c, align_bytes=64)
+            nc.vector.quantize_mx(out=z_codes[:].bitcast(FP8X4), scales=z_scale[:], in_=z16[:])
+            per_bank = 2 if last else S // width
+            for b in range(N // P // per_bank):
+                acc = bank(OUT_BANKS[c][b])
+                for a in range(per_bank):
+                    cols = slice((per_bank * b + a) * P, (per_bank * b + a + 1) * P)
+                    nc.tensor.matmul_mx(out=acc[:, a * width : (a + 1) * width], lhsT=w2_codes[:, cols].bitcast(FP8X4), lhsT_scale=w2_scale[:, cols],
+                                        rhs=z_codes[:].bitcast(FP8X4), rhs_scale=z_scale[:], start=True, stop=True)
+                result = keep.tile([P, per_bank, width], F32, name="result_%d_%d" % (c, b), align_bytes=64)
+                evacuate = nc.vector.tensor_copy if (last and b == 1) else nc.scalar.copy
+                evacuate(result[:].rearrange("p a n -> p (a n)"), acc[:, 0 : per_bank * width])
+                nc.sync.dma_start(out[per_bank * b * P : per_bank * (b + 1) * P, cells].rearrange("(a p) n -> p a n", p=P), result[:])
+            first = first + width

@@ -2,7 +2,6 @@ import math
 from contextlib import ExitStack
 
 import concourse.mybir as mybir
-from concourse.masks import make_identity
 
 F32 = mybir.dt.float32
 BF16 = mybir.dt.bfloat16
@@ -18,11 +17,7 @@ K, T, S, N, H = 512, 2048, 512, 512, 512
 P = 128
 PACK = 4
 LIST_ROWS = 16
-SUM_BANKS = ((1, 2), (0, 3), (5, 4))
-BACK_BANKS = (6, 7, 3)
-OUT_BANKS = ((1, 2), (0,), (5, 6))
 CHUNKS = (256, 128, 128)
-SIGMOID_PAIR = 1
 FLOPS = 2 * K * H * S + 2 * H * N * S
 
 
@@ -41,137 +36,119 @@ def tile_picked_fhn8_none_p_kernel(tc, x_words, x_scales, w1, rec, gn, w2, offs,
         east_sb = keep.tile([P, S // LIST_ROWS], U16, name="east_sb")
         xw_table = head.tile([P, T], U32, name="xw_table", offset=0, align_bytes=64)
         xs_table = keep.tile([P, T], U8, name="xs_table", tag="xs_then_w1", align_bytes=64)
-        gain = keep.tile([P, PACK], F32, name="gain", tag="w_raw", align_bytes=64)
+        w1_raw = keep.tile([P, PACK, H], F32, name="w1_raw", align_bytes=64)
+        gain = keep.tile([P, PACK], F32, name="gain")
 
         nc.vector.memset(xs_table[:].bitcast(I32), 0)
-        nc.sync.dma_start(gain[:], gn.rearrange("(p t) o -> p (t o)", t=PACK))
+        nc.gpsimd.dma_start(gain[:], gn.rearrange("(p t) o -> p (t o)", t=PACK))
         nc.sync.dma_start(offs_sb[:], offs)
+        nc.sync.dma_start(west_sb[:], west)
         nc.sync.dma_start(xw_table[:].bitcast(I32), x_words[0].rearrange("p n t -> p (n t)").bitcast(I32))
         for q in range(4):
             nc.scalar.dma_start(xs_table[32 * q : 32 * q + 4, :].bitcast(I32), x_scales[0, 4 * q : 4 * q + 4, :].bitcast(I32))
-        nc.sync.dma_start(west_sb[:], west)
+        nc.sync.dma_start(w1_raw[:], w1.rearrange("(p j) c -> p j c", j=PACK))
+        w2_raw = keep.tile([P, PACK, N], F32, name="w2_raw", align_bytes=64)
+        nc.sync.dma_start(w2_raw[:], w2.rearrange("(p j) c -> p j c", j=PACK))
         nc.sync.dma_start(east_sb[:], east)
 
-        ident = keep.tile([P, P], F32, name="ident", align_bytes=64)
-        make_identity(nc, ident[:])
+        seed = keep.tile([P, 1], F32, name="seed")
+        nc.vector.memset(seed[:], 0.0)
         warm = keep.tile([P, 1], F32, name="warm")
-        nc.scalar.activation(warm[:], ident[:, 0:1], ACT.Sigmoid)
+        nc.scalar.activation(warm[:], seed[:], ACT.Sigmoid)
+        gain_quarter = keep.tile([P, PACK], F32, name="gain_quarter")
+        gain_half = keep.tile([P, 2, PACK], F32, name="gain_half")
+        nc.scalar.activation(gain_quarter[:], gain[:], ACT.Copy, scale=0.25)
+        nc.scalar.activation(gain_half[:, 0, :], gain[:], ACT.Copy, scale=0.5)
+        nc.scalar.activation(gain_half[:, 1, :], gain[:], ACT.Copy, scale=-0.5)
 
         x_codes = keep.tile([P, S], U32, name="x_codes", align_bytes=64)
         nc.vector.tensor_copy(x_codes[:], xw_table[:].indirect(offs_sb[:]))
         x_scale = head.tile([P, S], U8, name="x_scale", offset=0, align_bytes=64)
         nc.vector.tensor_copy(x_scale[:], xs_table[:].indirect(offs_sb[:]))
 
-        def transpose_into(dst, src, start, stop):
-            nc.tensor.matmul(dst, lhsT=src, rhs=ident[:], start=start, stop=stop, is_transpose=True)
-
-        weight = [2.0 if t // 2 == SIGMOID_PAIR else 1.0 for t in range(PACK)]
-        gain_bank = bank(0)
-        for t in range(PACK):
-            transpose_into(gain_bank[:, t * P : (t + 1) * P], gain[:, t : t + 1].to_broadcast([P, P]), True, True)
-        w1_raw = keep.tile([P, PACK, H], F32, name="w1_raw", tag="w_raw", align_bytes=64)
-        nc.sync.dma_start(w1_raw[:], w1.rearrange("(p j) c -> p j c", j=PACK))
         rec_all = head.tile([P, PACK, S], F32, name="rec_all", offset=S, align_bytes=64)
         rec_rows = rec.rearrange("(p t) s -> p t s", t=PACK)
         for t in range(PACK):
             nc.sync.dma_start(rec_all[:, t, :], rec_rows[:, t, :])
-        rec_sb = [rec_all[:, t, :] for t in range(PACK)]
-
-        gain_row = keep.tile([P, 2, 2, P, 2], F32, name="gain_row", align_bytes=64)
-        for t in range(PACK):
-            nc.scalar.activation(gain_row[:, t // 2, :, :, t % 2], gain_bank[:, t * P : (t + 1) * P].unsqueeze(1).to_broadcast([P, 2, P]),
-                                 ACT.Copy, scale=-1.0 / weight[t])
 
         w1_cols = w1_raw[:].rearrange("p j (m t) -> p m j t", t=PACK)
-        y, ysq, cubic = [], [], []
-        logit = {}
-        for t in range(PACK):
-            if t % 2 == 0:
-                w1_pair = keep.tile([P, 2, P, PACK], BF16, name="w1_pair_%d" % t, tag="xs_then_w1", align_bytes=64)
-                nc.vector.tensor_copy(w1_pair[:].rearrange("p t m j -> p m j t"), w1_cols[:, :, :, t : t + 2])
-            codes = keep.tile([P, P], U32, name="w1_codes_%d" % t, align_bytes=64)
-            scale = keep.tile([P, P], U8, name="w1_scale_%d" % t, align_bytes=64)
-            nc.vector.quantize_mx(out=codes[:].bitcast(FP8X4), scales=scale[:],
-                                  in_=w1_pair[:, t % 2].rearrange("p m j -> p (m j)"))
-            acc = bank(1 + t)
-            nc.tensor.matmul_mx(out=acc[:], lhsT=codes[:].bitcast(FP8X4), lhsT_scale=scale[:],
-                                rhs=x_codes[:].bitcast(FP8X4), rhs_scale=x_scale[:], start=True, stop=True)
-            y.append(keep.tile([P, S], F32, name="y_%d" % t, align_bytes=64))
-            ysq.append(keep.tile([P, S], F32, name="ysq_%d" % t, tag="ysq_%d" % t, align_bytes=64))
-            nc.scalar.activation(y[t][:], acc[:], ACT.Tanh)
-            nc.scalar.activation(ysq[t][:], y[t][:], ACT.Square, scale=math.sqrt(0.3125 * weight[t]))
-            if t // 2 == SIGMOID_PAIR:
-                logit[t] = keep.tile([P, S], F32, name="logit_%d" % t, align_bytes=64)
-                nc.scalar.activation(logit[t][:], acc[:], ACT.Copy, scale=-2.0)
+        w1_low = keep.tile([P, 2, P, PACK], BF16, name="w1_low", tag="xs_then_w1", align_bytes=64)
+        w1_high = keep.tile([P, 2, P, PACK], BF16, name="w1_high", align_bytes=64)
+        nc.vector.tensor_copy(w1_low[:].rearrange("p t m j -> p m j t"), w1_cols[:, :, :, 0:2])
+        nc.scalar.copy(w1_high[:].rearrange("p t m j -> p m j t"), w1_cols[:, :, :, 2:4])
 
-        w2_raw = keep.tile([P, PACK, N], F32, name="w2_raw", tag="w_raw", align_bytes=64)
-        nc.sync.dma_start(w2_raw[:], w2.rearrange("(p j) c -> p j c", j=PACK))
+        y, yg, ysq, logit = [], [], [], {}
+        for pair, grouped in enumerate((w1_low, w1_high)):
+            codes = keep.tile([P, 2, P], U32, name="w1_codes_%d" % pair, tag=("w1_codes", "xs_then_w1")[pair], align_bytes=64)
+            scale = keep.tile([P, 2, P], U8, name="w1_scale_%d" % pair, align_bytes=64)
+            for e in range(2):
+                t = 2 * pair + e
+                nc.vector.quantize_mx(out=codes[:, e].bitcast(FP8X4), scales=scale[:, e], in_=grouped[:, e].rearrange("p m j -> p (m j)"))
+                acc = bank(t)
+                nc.tensor.matmul_mx(out=acc[:], lhsT=codes[:, e].bitcast(FP8X4), lhsT_scale=scale[:, e],
+                                    rhs=x_codes[:].bitcast(FP8X4), rhs_scale=x_scale[:], start=True, stop=True)
+                y.append(keep.tile([P, S], F32, name="y_%d" % t, align_bytes=64))
+                yg.append(keep.tile([P, S], F32, name="yg_%d" % t, align_bytes=64))
+                ysq.append(keep.tile([P, S], F32, name="ysq_%d" % t, align_bytes=64))
+                nc.scalar.activation(y[t][:], acc[:], ACT.Tanh)
+                nc.scalar.activation(ysq[t][:], y[t][:], ACT.Square, scale=math.sqrt(1.25))
+                if pair == 0:
+                    nc.vector.tensor_scalar(yg[t][:], y[t][:], gain_quarter[:, t : t + 1], None, ALU.mult)
+                else:
+                    nc.scalar.activation(yg[t][:], y[t][:], ACT.Copy, scale=gain_quarter[:, t : t + 1])
+                    logit[t] = keep.tile([P, S], F32, name="logit_%d" % t, align_bytes=64)
+                    nc.scalar.activation(logit[t][:], acc[:], ACT.Copy, scale=2.0)
+
         w2_codes = keep.tile([P, N], U32, name="w2_codes", align_bytes=64)
         w2_scale = keep.tile([P, N], U8, name="w2_scale", align_bytes=64)
+        w2_grouped = keep.tile([P, N, PACK], BF16, name="w2_grouped", align_bytes=64)
+        nc.vector.tensor_copy(w2_grouped[:].rearrange("p (c i) j -> p c j i", i=4), w2_raw[:].rearrange("p j (c i) -> p c j i", i=4))
+        nc.vector.quantize_mx(out=w2_codes[:].bitcast(FP8X4), scales=w2_scale[:], in_=w2_grouped[:].rearrange("p c j -> p (c j)"))
 
-        def prepare_w2():
-            grouped = keep.tile([P, N, PACK], BF16, name="w2_grouped", align_bytes=64)
-            nc.vector.tensor_copy(grouped[:].rearrange("p (c i) j -> p c j i", i=4), w2_raw[:].rearrange("p j (c i) -> p c j i", i=4))
-            nc.vector.quantize_mx(out=w2_codes[:].bitcast(FP8X4), scales=w2_scale[:], in_=grouped[:].rearrange("p c j -> p (c j)"))
+        firsts = [sum(CHUNKS[:c]) for c in range(len(CHUNKS))]
+        local, z32 = [], {}
 
-        first = 0
-        for c, width in enumerate(CHUNKS):
+        def local_term(t):
+            cubic = keep.tile([P, S], F32, name="cubic_%d" % t, align_bytes=64)
+            local.append(keep.tile([P, S], F32, name="local_%d" % t, align_bytes=64))
+            halves = (slice(0, S // 2), slice(S // 2, S))
+            for cols in halves:
+                nc.vector.scalar_tensor_tensor(cubic[:, cols], ysq[t][:, cols], 4.0, yg[t][:, cols], ALU.subtract, ALU.mult)
+            for cols in halves:
+                nc.vector.scalar_tensor_tensor(local[t][:, cols], rec_all[:, t, cols], gain[:, t : t + 1], cubic[:, cols], ALU.mult, ALU.add)
+
+        cells = [slice(first, first + width) for first, width in zip(firsts, CHUNKS)]
+        entries = [slice(first // LIST_ROWS, (first + width) // LIST_ROWS) for first, width in zip(firsts, CHUNKS)]
+
+        def neighbours(c, half_tag, z32_tag):
+            width = CHUNKS[c]
+            near = keep.tile([P, 2, 2, width], F32, name="near_%d" % c, align_bytes=64)
+            half = keep.tile([P, PACK, width], F32, name="half_%d" % c, tag=half_tag, align_bytes=64)
+            z32[c] = keep.tile([P, PACK, width], F32, name="z32_%d" % c, tag=z32_tag, align_bytes=64)
+            for t in (2, 3):
+                nc.scalar.activation(near[:, t - 2, 0, :], logit[t][:].indirect(west_sb[:, entries[c]]), ACT.Sigmoid)
+                nc.scalar.activation(near[:, t - 2, 1, :], logit[t][:].indirect(east_sb[:, entries[c]]), ACT.Sigmoid, scale=-1.0)
+            for t in (0, 1):
+                nc.vector.tensor_tensor(half[:, t, :], yg[t][:].indirect(west_sb[:, entries[c]]), local[t][:, cells[c]], ALU.subtract)
+            for t in (0, 1):
+                nc.vector.tensor_tensor(z32[c][:, t, :], yg[t][:].indirect(east_sb[:, entries[c]]), half[:, t, :], ALU.add)
+            for t in (2, 3):
+                nc.vector.scalar_tensor_tensor(half[:, t, :], near[:, t - 2, 0, :], gain_half[:, 0, t : t + 1], local[t][:, cells[c]], ALU.mult, ALU.subtract)
+            for t in (2, 3):
+                nc.vector.scalar_tensor_tensor(z32[c][:, t, :], near[:, t - 2, 1, :], gain_half[:, 1, t : t + 1], half[:, t, :], ALU.mult, ALU.add)
+
+        def second_product(c, out_banks):
+            width = CHUNKS[c]
             last = c == len(CHUNKS) - 1
-            blocks = width // P
-            cells = slice(first, first + width)
-            entries = slice(first // LIST_ROWS, (first + width) // LIST_ROWS)
-            if c == 0:
-                tags = ("near_0_0", "ysq_0", "near_0_2", "near_0_3")
-                near = [keep.tile([P, 2, width], F32, name="near_0_%d" % t, tag=tags[t], align_bytes=64)[:] for t in range(PACK)]
-            else:
-                near_low = keep.tile([P, 2, 2, width], F32, name="near_low_%d" % c, tag=(None, "ysq_3", "zt_0_1")[c], align_bytes=64)
-                near_top = keep.tile([P, 2, 2, width], F32, name="near_top_%d" % c, align_bytes=64)
-                near = [near_low[:, 0], near_low[:, 1], near_top[:, 0], near_top[:, 1]]
-            zt = {}
-            for u in ((1, 0) if last else (0, 1)):
-                sums = bank(SUM_BANKS[c][u])
-                early, late = [], []
-                for e in range(2):
-                    t = 2 * u + e
-                    for side, lst in enumerate((west_sb, east_sb)):
-                        if u == SIGMOID_PAIR:
-                            nc.scalar.activation(near[t][:, side, :], logit[t][:].indirect(lst[:, entries]), ACT.Sigmoid)
-                        else:
-                            nc.vector.tensor_scalar(near[t][:, side, :], y[t][:].indirect(lst[:, entries]), -0.25, 0.0, ALU.mult, ALU.add)
-                    if c == 0:
-                        cubic.append(keep.tile([P, S], F32, name="cubic_%d" % t, align_bytes=64))
-                        nc.vector.scalar_tensor_tensor(cubic[t][:], ysq[t][:], weight[t], y[t][:], ALU.subtract, ALU.mult)
-                    places = [(sums[:, (e * blocks + b) * P : (e * blocks + b + 1) * P], slice(b * P, (b + 1) * P),
-                               slice(first + b * P, first + (b + 1) * P)) for b in range(blocks)]
-                    recs = [(dst, rec_sb[t][:, own]) for dst, here, own in places] * int(weight[t])
-                    cubics = [(dst, cubic[t][:, own]) for dst, here, own in places]
-                    gathered = [(dst, near[t][:, side, here]) for side in range(2) for dst, here, own in places]
-                    if c == 0 and u != SIGMOID_PAIR:
-                        early, late = early + recs, late + gathered + cubics
-                    else:
-                        early, late = early + recs + cubics, late + gathered
-                terms = early + late
-                for i, (dst, term) in enumerate(terms):
-                    transpose_into(dst, term, i == 0, i == len(terms) - 1)
-                zt[u] = keep.tile([P, width, 2], BF16, name="zt_%d_%d" % (c, u), tag="zt_%d_%d" % (c, u), align_bytes=64)
-                nc.vector.scalar_tensor_tensor(zt[u][:], sums[:, 0 : 2 * width].rearrange("q (e n) -> q n e", e=2), float(u),
-                                               gain_row[:, u, 0:blocks].rearrange("q b p e -> q (b p) e"), ALU.subtract, ALU.mult)
-            if c == 0:
-                prepare_w2()
-            back = bank(BACK_BANKS[c])
-            for u in zt:
-                for b in range(blocks):
-                    words = zt[u][:, b * P : (b + 1) * P].rearrange("q p e -> q (p e)").bitcast(F32)
-                    transpose_into(back[:, (u * blocks + b) * P : (u * blocks + b + 1) * P], words, True, True)
-            z16 = keep.tile([P, width * PACK], BF16, name="z16_%d" % c, tag="z16_%d" % c, align_bytes=64)
-            unpack = nc.vector.tensor_copy if last else nc.scalar.copy
-            unpack(z16[:].bitcast(F32).rearrange("p (n u) -> p n u", u=2), back[:, 0 : 2 * width].rearrange("p (u n) -> p n u", u=2))
+            z16 = keep.tile([P, width, PACK], BF16, name="z16_%d" % c, tag="z16_%d" % c, align_bytes=64)
+            interleave = nc.vector.tensor_copy if last else nc.scalar.copy
+            interleave(z16[:].rearrange("p (c i) t -> p c t i", i=4), z32[c][:].rearrange("p t (c i) -> p c t i", i=4))
             z_codes = keep.tile([P, width], U32, name="z_codes_%d" % c, align_bytes=64)
             z_scale = keep.tile([P, width], U8, name="z_scale_%d" % c, align_bytes=64)
-            nc.vector.quantize_mx(out=z_codes[:].bitcast(FP8X4), scales=z_scale[:], in_=z16[:])
-            per_bank = 2 if last else S // width
-            for b in range(N // P // per_bank):
-                acc = bank(OUT_BANKS[c][b])
+            nc.vector.quantize_mx(out=z_codes[:].bitcast(FP8X4), scales=z_scale[:], in_=z16[:].rearrange("p c t -> p (c t)"))
+            per_bank = N // P // len(out_banks)
+            for b, number in enumerate(out_banks):
+                acc = bank(number)
                 for a in range(per_bank):
                     cols = slice((per_bank * b + a) * P, (per_bank * b + a + 1) * P)
                     nc.tensor.matmul_mx(out=acc[:, a * width : (a + 1) * width], lhsT=w2_codes[:, cols].bitcast(FP8X4), lhsT_scale=w2_scale[:, cols],
@@ -179,5 +156,13 @@ def tile_picked_fhn8_none_p_kernel(tc, x_words, x_scales, w1, rec, gn, w2, offs,
                 result = keep.tile([P, per_bank, width], F32, name="result_%d_%d" % (c, b), align_bytes=64)
                 evacuate = nc.vector.tensor_copy if (last and b == 1) else nc.scalar.copy
                 evacuate(result[:].rearrange("p a n -> p (a n)"), acc[:, 0 : per_bank * width])
-                nc.sync.dma_start(out[per_bank * b * P : per_bank * (b + 1) * P, cells].rearrange("(a p) n -> p a n", p=P), result[:])
-            first = first + width
+                nc.sync.dma_start(out[per_bank * b * P : per_bank * (b + 1) * P, firsts[c] : firsts[c] + width].rearrange("(a p) n -> p a n", p=P), result[:])
+
+        for t in range(PACK):
+            local_term(t)
+        neighbours(0, "half", "z32_0")
+        second_product(0, (4, 5))
+        neighbours(1, "half", "z32_1")
+        second_product(1, (6,))
+        neighbours(2, "z16_0", "z16_1")
+        second_product(2, (7, 0))

@@ -2,6 +2,7 @@ import math
 from contextlib import ExitStack
 
 import concourse.mybir as mybir
+from concourse.masks import make_identity
 
 F32 = mybir.dt.float32
 BF16 = mybir.dt.bfloat16
@@ -17,7 +18,12 @@ K, T, S, N, H = 512, 2048, 512, 512, 512
 P = 128
 PACK = 4
 LIST_ROWS = 16
-CHUNKS = (256, 128, 128)
+CHUNKS = (256, 256)
+SUM_BANKS = (5, 6, 7, 0)
+BACK_BANKS = (1, 2)
+OUT_BANKS = ((3, 4, 5, 6), (7, 0, 1, 3))
+ON_VECTOR = ((0, 1), (0, 3), (1, 1), (1, 3))
+WEIGHT = (2.0, 2.0, 4.0, 4.0)
 FLOPS = 2 * K * H * S + 2 * H * N * S
 
 
@@ -36,11 +42,11 @@ def tile_picked_fhn8_none_p_kernel(tc, x_words, x_scales, w1, rec, gn, w2, offs,
         east_sb = keep.tile([P, S // LIST_ROWS], U16, name="east_sb")
         xw_table = head.tile([P, T], U32, name="xw_table", offset=0, align_bytes=64)
         xs_table = keep.tile([P, T], U8, name="xs_table", tag="xs_then_w1", align_bytes=64)
-        w1_raw = keep.tile([P, PACK, H], F32, name="w1_raw", align_bytes=64)
+        w1_raw = keep.tile([P, PACK, H], F32, name="w1_raw", tag="w1_then_rec", align_bytes=64)
         gain = keep.tile([P, PACK], F32, name="gain")
 
         nc.vector.memset(xs_table[:].bitcast(I32), 0)
-        nc.gpsimd.dma_start(gain[:], gn.rearrange("(p t) o -> p (t o)", t=PACK))
+        nc.sync.dma_start(gain[:], gn.rearrange("(p t) o -> p (t o)", t=PACK))
         nc.sync.dma_start(offs_sb[:], offs)
         nc.sync.dma_start(west_sb[:], west)
         nc.sync.dma_start(xw_table[:].bitcast(I32), x_words[0].rearrange("p n t -> p (n t)").bitcast(I32))
@@ -51,25 +57,28 @@ def tile_picked_fhn8_none_p_kernel(tc, x_words, x_scales, w1, rec, gn, w2, offs,
         nc.sync.dma_start(w2_raw[:], w2.rearrange("(p j) c -> p j c", j=PACK))
         nc.sync.dma_start(east_sb[:], east)
 
+        ident = keep.tile([P, P], F32, name="ident", align_bytes=64)
+        make_identity(nc, ident[:])
         seed = keep.tile([P, 1], F32, name="seed")
         nc.vector.memset(seed[:], 0.0)
         warm = keep.tile([P, 1], F32, name="warm")
         nc.scalar.activation(warm[:], seed[:], ACT.Sigmoid)
-        gain_quarter = keep.tile([P, PACK], F32, name="gain_quarter")
-        gain_half = keep.tile([P, 2, PACK], F32, name="gain_half")
-        nc.scalar.activation(gain_quarter[:], gain[:], ACT.Copy, scale=0.25)
-        nc.scalar.activation(gain_half[:, 0, :], gain[:], ACT.Copy, scale=0.5)
-        nc.scalar.activation(gain_half[:, 1, :], gain[:], ACT.Copy, scale=-0.5)
+
+        def transpose_into(dst, src, start, stop):
+            nc.tensor.matmul(dst, lhsT=src, rhs=ident[:], start=start, stop=stop, is_transpose=True)
+
+        gain_bank = bank(0)
+        for t in range(PACK):
+            transpose_into(gain_bank[:, t * P : (t + 1) * P], gain[:, t : t + 1].to_broadcast([P, P]), True, True)
+        gain_row = keep.tile([P, 2, P, 2], F32, name="gain_row", align_bytes=64)
+        for u in range(2):
+            planes = gain_bank[:, 2 * u * P : (2 * u + 2) * P].rearrange("q (e p) -> q p e", e=2)
+            nc.scalar.activation(gain_row[:, u], planes, ACT.Copy, scale=-1.0 / WEIGHT[2 * u])
 
         x_codes = keep.tile([P, S], U32, name="x_codes", align_bytes=64)
         nc.vector.tensor_copy(x_codes[:], xw_table[:].indirect(offs_sb[:]))
         x_scale = head.tile([P, S], U8, name="x_scale", offset=0, align_bytes=64)
         nc.vector.tensor_copy(x_scale[:], xs_table[:].indirect(offs_sb[:]))
-
-        rec_all = head.tile([P, PACK, S], F32, name="rec_all", offset=S, align_bytes=64)
-        rec_rows = rec.rearrange("(p t) s -> p t s", t=PACK)
-        for t in range(PACK):
-            nc.sync.dma_start(rec_all[:, t, :], rec_rows[:, t, :])
 
         w1_cols = w1_raw[:].rearrange("p j (m t) -> p m j t", t=PACK)
         w1_low = keep.tile([P, 2, P, PACK], BF16, name="w1_low", tag="xs_then_w1", align_bytes=64)
@@ -77,27 +86,28 @@ def tile_picked_fhn8_none_p_kernel(tc, x_words, x_scales, w1, rec, gn, w2, offs,
         nc.vector.tensor_copy(w1_low[:].rearrange("p t m j -> p m j t"), w1_cols[:, :, :, 0:2])
         nc.scalar.copy(w1_high[:].rearrange("p t m j -> p m j t"), w1_cols[:, :, :, 2:4])
 
-        y, yg, ysq, logit = [], [], [], {}
+        rec_all = head.tile([P, PACK, S], F32, name="rec_all", offset=S, align_bytes=64)
+        rec_rows = rec.rearrange("(p t) s -> p t s", t=PACK)
+        for t in range(PACK):
+            nc.sync.dma_start(rec_all[:, t, :], rec_rows[:, t, :])
+
+        y, ysq, logit = [], [], {}
         for pair, grouped in enumerate((w1_low, w1_high)):
             codes = keep.tile([P, 2, P], U32, name="w1_codes_%d" % pair, tag=("w1_codes", "xs_then_w1")[pair], align_bytes=64)
             scale = keep.tile([P, 2, P], U8, name="w1_scale_%d" % pair, align_bytes=64)
             for e in range(2):
                 t = 2 * pair + e
                 nc.vector.quantize_mx(out=codes[:, e].bitcast(FP8X4), scales=scale[:, e], in_=grouped[:, e].rearrange("p m j -> p (m j)"))
-                acc = bank(t)
+                acc = bank(1 + t)
                 nc.tensor.matmul_mx(out=acc[:], lhsT=codes[:, e].bitcast(FP8X4), lhsT_scale=scale[:, e],
                                     rhs=x_codes[:].bitcast(FP8X4), rhs_scale=x_scale[:], start=True, stop=True)
                 y.append(keep.tile([P, S], F32, name="y_%d" % t, align_bytes=64))
-                yg.append(keep.tile([P, S], F32, name="yg_%d" % t, align_bytes=64))
-                ysq.append(keep.tile([P, S], F32, name="ysq_%d" % t, align_bytes=64))
-                nc.scalar.activation(y[t][:], acc[:], ACT.Tanh)
-                nc.scalar.activation(ysq[t][:], y[t][:], ACT.Square, scale=math.sqrt(1.25))
+                ysq.append(keep.tile([P, S], F32, name="ysq_%d" % t, tag="ysq_%d" % t, align_bytes=64))
+                nc.scalar.activation(y[t][:], acc[:], ACT.Tanh, scale=(1.0, -1.0)[pair])
+                nc.scalar.activation(ysq[t][:], y[t][:], ACT.Square, scale=math.sqrt(0.3125 * WEIGHT[t]))
                 if pair == 0:
-                    nc.vector.tensor_scalar(yg[t][:], y[t][:], gain_quarter[:, t : t + 1], None, ALU.mult)
-                else:
-                    nc.scalar.activation(yg[t][:], y[t][:], ACT.Copy, scale=gain_quarter[:, t : t + 1])
                     logit[t] = keep.tile([P, S], F32, name="logit_%d" % t, align_bytes=64)
-                    nc.scalar.activation(logit[t][:], acc[:], ACT.Copy, scale=2.0)
+                    nc.scalar.activation(logit[t][:], acc[:], ACT.Copy, scale=-2.0)
 
         w2_codes = keep.tile([P, N], U32, name="w2_codes", align_bytes=64)
         w2_scale = keep.tile([P, N], U8, name="w2_scale", align_bytes=64)
@@ -106,63 +116,90 @@ def tile_picked_fhn8_none_p_kernel(tc, x_words, x_scales, w1, rec, gn, w2, offs,
         nc.vector.quantize_mx(out=w2_codes[:].bitcast(FP8X4), scales=w2_scale[:], in_=w2_grouped[:].rearrange("p c j -> p (c j)"))
 
         firsts = [sum(CHUNKS[:c]) for c in range(len(CHUNKS))]
-        local, z32 = [], {}
-
-        def local_term(t):
-            cubic = keep.tile([P, S], F32, name="cubic_%d" % t, align_bytes=64)
-            local.append(keep.tile([P, S], F32, name="local_%d" % t, align_bytes=64))
-            halves = (slice(0, S // 2), slice(S // 2, S))
-            for cols in halves:
-                nc.vector.scalar_tensor_tensor(cubic[:, cols], ysq[t][:, cols], 4.0, yg[t][:, cols], ALU.subtract, ALU.mult)
-            for cols in halves:
-                nc.vector.scalar_tensor_tensor(local[t][:, cols], rec_all[:, t, cols], gain[:, t : t + 1], cubic[:, cols], ALU.mult, ALU.add)
-
         cells = [slice(first, first + width) for first, width in zip(firsts, CHUNKS)]
         entries = [slice(first // LIST_ROWS, (first + width) // LIST_ROWS) for first, width in zip(firsts, CHUNKS)]
+        halves = (slice(0, S // 2), slice(S // 2, S))
+        blocks = [slice(b * P, (b + 1) * P) for b in range(S // P)]
 
-        def neighbours(c, half_tag, z32_tag):
-            width = CHUNKS[c]
-            near = keep.tile([P, 2, 2, width], F32, name="near_%d" % c, align_bytes=64)
-            half = keep.tile([P, PACK, width], F32, name="half_%d" % c, tag=half_tag, align_bytes=64)
-            z32[c] = keep.tile([P, PACK, width], F32, name="z32_%d" % c, tag=z32_tag, align_bytes=64)
-            for t in (2, 3):
-                nc.scalar.activation(near[:, t - 2, 0, :], logit[t][:].indirect(west_sb[:, entries[c]]), ACT.Sigmoid)
-                nc.scalar.activation(near[:, t - 2, 1, :], logit[t][:].indirect(east_sb[:, entries[c]]), ACT.Sigmoid, scale=-1.0)
-            for t in (0, 1):
-                nc.vector.tensor_tensor(half[:, t, :], yg[t][:].indirect(west_sb[:, entries[c]]), local[t][:, cells[c]], ALU.subtract)
-            for t in (0, 1):
-                nc.vector.tensor_tensor(z32[c][:, t, :], yg[t][:].indirect(east_sb[:, entries[c]]), half[:, t, :], ALU.add)
-            for t in (2, 3):
-                nc.vector.scalar_tensor_tensor(half[:, t, :], near[:, t - 2, 0, :], gain_half[:, 0, t : t + 1], local[t][:, cells[c]], ALU.mult, ALU.subtract)
-            for t in (2, 3):
-                nc.vector.scalar_tensor_tensor(z32[c][:, t, :], near[:, t - 2, 1, :], gain_half[:, 1, t : t + 1], half[:, t, :], ALU.mult, ALU.add)
+        rec_k, cubic, near = [], [], {}
 
-        def second_product(c, out_banks):
+        def west_plus_rec(t, h, dst):
+            nc.vector.tensor_tensor(dst, y[t][:].indirect(west_sb[:, 16 * h : 16 * h + 16]), rec_k[t][:, halves[h]], ALU.add)
+
+        def east_minus_cubic(t, h, dst):
+            nc.vector.tensor_tensor(dst, y[t][:].indirect(east_sb[:, 16 * h : 16 * h + 16]), cubic[t][:, halves[h]], ALU.subtract)
+
+        for t in range(PACK):
+            rec_k.append(keep.tile([P, S], F32, name="rec_k_%d" % t, align_bytes=64))
+            nc.vector.tensor_scalar(rec_k[t][:], rec_all[:, t, :], WEIGHT[t], (-1.0, 0.0)[t // 2], ALU.mult, ALU.add)
+        for t in range(PACK):
+            cubic.append(keep.tile([P, S], F32, name="cubic_%d" % t, align_bytes=64))
+            nc.vector.scalar_tensor_tensor(cubic[t][:], ysq[t][:], WEIGHT[t], y[t][:], ALU.subtract, ALU.mult)
+        west_sum = keep.tile([P, 2, S], F32, name="west_sum", align_bytes=64)
+        east_sum = keep.tile([P, 2, S], F32, name="east_sum", align_bytes=64)
+        for h in range(2):
+            for t in (2, 3):
+                west_plus_rec(t, h, west_sum[:, t - 2, halves[h]])
+            for t in (2, 3):
+                east_minus_cubic(t, h, east_sum[:, t - 2, halves[h]])
+        for t in (0, 1):
+            near[t] = keep.tile([P, 2, S], F32, name="near_%d" % t, align_bytes=64)
+        for c in range(len(CHUNKS)):
+            for t in (0, 1):
+                for side, lst in enumerate((west_sb, east_sb)):
+                    nc.scalar.activation(near[t][:, side, cells[c]], logit[t][:].indirect(lst[:, entries[c]]), ACT.Sigmoid)
+
+        def quantise_z(c):
             width = CHUNKS[c]
-            last = c == len(CHUNKS) - 1
-            z16 = keep.tile([P, width, PACK], BF16, name="z16_%d" % c, tag="z16_%d" % c, align_bytes=64)
-            interleave = nc.vector.tensor_copy if last else nc.scalar.copy
-            interleave(z16[:].rearrange("p (c i) t -> p c t i", i=4), z32[c][:].rearrange("p t (c i) -> p c t i", i=4))
+            z16 = keep.tile([P, width * PACK], BF16, name="z16_%d" % c, align_bytes=64)
+            nc.scalar.copy(z16[:].bitcast(F32).rearrange("p (n u) -> p n u", u=2), back[c][:, 0 : 2 * width].rearrange("p (u n) -> p n u", u=2))
             z_codes = keep.tile([P, width], U32, name="z_codes_%d" % c, align_bytes=64)
             z_scale = keep.tile([P, width], U8, name="z_scale_%d" % c, align_bytes=64)
-            nc.vector.quantize_mx(out=z_codes[:].bitcast(FP8X4), scales=z_scale[:], in_=z16[:].rearrange("p c t -> p (c t)"))
-            per_bank = N // P // len(out_banks)
-            for b, number in enumerate(out_banks):
+            nc.vector.quantize_mx(out=z_codes[:].bitcast(FP8X4), scales=z_scale[:], in_=z16[:])
+            return z_codes, z_scale
+
+        def second_product(c, z_codes, z_scale):
+            width = CHUNKS[c]
+            per_bank = N // P // len(OUT_BANKS[c])
+            for b, number in enumerate(OUT_BANKS[c]):
                 acc = bank(number)
                 for a in range(per_bank):
                     cols = slice((per_bank * b + a) * P, (per_bank * b + a + 1) * P)
                     nc.tensor.matmul_mx(out=acc[:, a * width : (a + 1) * width], lhsT=w2_codes[:, cols].bitcast(FP8X4), lhsT_scale=w2_scale[:, cols],
                                         rhs=z_codes[:].bitcast(FP8X4), rhs_scale=z_scale[:], start=True, stop=True)
                 result = keep.tile([P, per_bank, width], F32, name="result_%d_%d" % (c, b), align_bytes=64)
-                evacuate = nc.vector.tensor_copy if (last and b == 1) else nc.scalar.copy
+                evacuate = nc.vector.tensor_copy if (c, b) in ON_VECTOR else nc.scalar.copy
                 evacuate(result[:].rearrange("p a n -> p (a n)"), acc[:, 0 : per_bank * width])
-                nc.sync.dma_start(out[per_bank * b * P : per_bank * (b + 1) * P, firsts[c] : firsts[c] + width].rearrange("(a p) n -> p a n", p=P), result[:])
+                nc.sync.dma_start(out[per_bank * b * P : per_bank * (b + 1) * P, cells[c]].rearrange("(a p) n -> p a n", p=P), result[:])
 
-        for t in range(PACK):
-            local_term(t)
-        neighbours(0, "half", "z32_0")
-        second_product(0, (4, 5))
-        neighbours(1, "half", "z32_1")
-        second_product(1, (6,))
-        neighbours(2, "z16_0", "z16_1")
-        second_product(2, (7, 0))
+        sums = [bank(number) for number in SUM_BANKS]
+
+        def add_term(t, term, where, start=False, stop=False):
+            for b in where:
+                transpose_into(sums[b][:, t * P : (t + 1) * P], term[:, blocks[b]], start, stop)
+
+        everywhere = range(len(blocks))
+        add_term(0, rec_k[0][:], everywhere, start=True)
+        add_term(1, rec_k[1][:], everywhere)
+        add_term(0, cubic[0][:], everywhere)
+        add_term(1, cubic[1][:], everywhere)
+        for t in (2, 3):
+            add_term(t, west_sum[:, t - 2, :], everywhere)
+        back = [bank(number) for number in BACK_BANKS]
+        for c in range(2):
+            here = (2 * c, 2 * c + 1)
+            for t in (0, 1):
+                for side in range(2):
+                    add_term(t, near[t][:, side, :], here)
+            add_term(2, east_sum[:, 0, :], here)
+            add_term(3, east_sum[:, 1, :], here, stop=True)
+        for c in range(2):
+            for b in (2 * c, 2 * c + 1):
+                zt = keep.tile([P, 2, P, 2], BF16, name="zt_%d" % b, align_bytes=64)
+                nc.vector.tensor_tensor(zt[:], sums[b][:].rearrange("q (u e p) -> q u p e", u=2, e=2), gain_row[:], ALU.mult)
+                for u in range(2):
+                    start = u * CHUNKS[c] + b % 2 * P
+                    transpose_into(back[c][:, start : start + P], zt[:, u].rearrange("q p e -> q (p e)").bitcast(F32), True, True)
+        z_mx = [quantise_z(c) for c in range(2)]
+        for c in range(2):
+            second_product(c, *z_mx[c])

@@ -22,8 +22,8 @@ CHUNKS = (256, 256)
 SUM_BANKS = (5, 6, 7, 0)
 BACK_BANKS = (1, 2)
 OUT_BANKS = ((3, 4, 5, 6), (7, 0, 1, 3))
-ON_VECTOR = ((0, 1), (0, 3), (1, 1), (1, 3))
-WEIGHT = (2.0, 2.0, 4.0, 4.0)
+ON_VECTOR = ((1, 1), (1, 3))
+WEIGHT = (1.0, 2.0, 1.0, 2.0)
 FLOPS = 2 * K * H * S + 2 * H * N * S
 
 
@@ -71,9 +71,9 @@ def tile_picked_fhn8_none_p_kernel(tc, x_words, x_scales, w1, rec, gn, w2, offs,
         for t in range(PACK):
             transpose_into(gain_bank[:, t * P : (t + 1) * P], gain[:, t : t + 1].to_broadcast([P, P]), True, True)
         gain_row = keep.tile([P, 2, P, 2], F32, name="gain_row", align_bytes=64)
-        for u in range(2):
-            planes = gain_bank[:, 2 * u * P : (2 * u + 2) * P].rearrange("q (e p) -> q p e", e=2)
-            nc.scalar.activation(gain_row[:, u], planes, ACT.Copy, scale=-1.0 / WEIGHT[2 * u])
+        for e in range(2):
+            planes = gain_bank[:].rearrange("q (u e p) -> q u e p", u=2, e=2)[:, :, e, :]
+            nc.scalar.activation(gain_row[:, :, :, e], planes, ACT.Copy, scale=-1.0 / WEIGHT[e])
 
         x_codes = keep.tile([P, S], U32, name="x_codes", align_bytes=64)
         nc.vector.tensor_copy(x_codes[:], xw_table[:].indirect(offs_sb[:]))
@@ -88,7 +88,7 @@ def tile_picked_fhn8_none_p_kernel(tc, x_words, x_scales, w1, rec, gn, w2, offs,
 
         rec_all = head.tile([P, PACK, S], F32, name="rec_all", offset=S, align_bytes=64)
         rec_rows = rec.rearrange("(p t) s -> p t s", t=PACK)
-        for t in range(PACK):
+        for t in (0, 2, 1, 3):
             nc.sync.dma_start(rec_all[:, t, :], rec_rows[:, t, :])
 
         y, ysq, logit = [], [], {}
@@ -103,9 +103,9 @@ def tile_picked_fhn8_none_p_kernel(tc, x_words, x_scales, w1, rec, gn, w2, offs,
                                     rhs=x_codes[:].bitcast(FP8X4), rhs_scale=x_scale[:], start=True, stop=True)
                 y.append(keep.tile([P, S], F32, name="y_%d" % t, align_bytes=64))
                 ysq.append(keep.tile([P, S], F32, name="ysq_%d" % t, tag="ysq_%d" % t, align_bytes=64))
-                nc.scalar.activation(y[t][:], acc[:], ACT.Tanh, scale=(1.0, -1.0)[pair])
+                nc.scalar.activation(y[t][:], acc[:], ACT.Tanh)
                 nc.scalar.activation(ysq[t][:], y[t][:], ACT.Square, scale=math.sqrt(0.3125 * WEIGHT[t]))
-                if pair == 0:
+                if e == 1:
                     logit[t] = keep.tile([P, S], F32, name="logit_%d" % t, align_bytes=64)
                     nc.scalar.activation(logit[t][:], acc[:], ACT.Copy, scale=-2.0)
 
@@ -121,31 +121,25 @@ def tile_picked_fhn8_none_p_kernel(tc, x_words, x_scales, w1, rec, gn, w2, offs,
         halves = (slice(0, S // 2), slice(S // 2, S))
         blocks = [slice(b * P, (b + 1) * P) for b in range(S // P)]
 
-        rec_k, cubic, near = [], [], {}
+        rec_k, cubic, near = {}, [], {}
 
-        def west_plus_rec(t, h, dst):
-            nc.vector.tensor_tensor(dst, y[t][:].indirect(west_sb[:, 16 * h : 16 * h + 16]), rec_k[t][:, halves[h]], ALU.add)
+        def vector_neighbours(t, tag):
+            near[t] = keep.tile([P, 2, S], F32, name="near_%d" % t, tag=tag, align_bytes=64)
+            for c in range(len(CHUNKS)):
+                for side, lst in enumerate((west_sb, east_sb)):
+                    nc.vector.tensor_scalar(near[t][:, side, cells[c]], y[t][:].indirect(lst[:, entries[c]]), -0.25, 0.0, ALU.mult, ALU.add)
 
-        def east_minus_cubic(t, h, dst):
-            nc.vector.tensor_tensor(dst, y[t][:].indirect(east_sb[:, 16 * h : 16 * h + 16]), cubic[t][:, halves[h]], ALU.subtract)
-
+        vector_neighbours(0, "near_0")
         for t in range(PACK):
-            rec_k.append(keep.tile([P, S], F32, name="rec_k_%d" % t, align_bytes=64))
-            nc.vector.tensor_scalar(rec_k[t][:], rec_all[:, t, :], WEIGHT[t], (-1.0, 0.0)[t // 2], ALU.mult, ALU.add)
-        for t in range(PACK):
+            if t % 2 == 1:
+                near[t] = keep.tile([P, 2, S], F32, name="near_%d" % t, align_bytes=64)
+                rec_k[t] = keep.tile([P, S], F32, name="rec_k_%d" % t, align_bytes=64)
+                nc.vector.tensor_scalar(rec_k[t][:], rec_all[:, t, :], 2.0, -1.0, ALU.mult, ALU.add)
             cubic.append(keep.tile([P, S], F32, name="cubic_%d" % t, align_bytes=64))
             nc.vector.scalar_tensor_tensor(cubic[t][:], ysq[t][:], WEIGHT[t], y[t][:], ALU.subtract, ALU.mult)
-        west_sum = keep.tile([P, 2, S], F32, name="west_sum", align_bytes=64)
-        east_sum = keep.tile([P, 2, S], F32, name="east_sum", align_bytes=64)
-        for h in range(2):
-            for t in (2, 3):
-                west_plus_rec(t, h, west_sum[:, t - 2, halves[h]])
-            for t in (2, 3):
-                east_minus_cubic(t, h, east_sum[:, t - 2, halves[h]])
-        for t in (0, 1):
-            near[t] = keep.tile([P, 2, S], F32, name="near_%d" % t, align_bytes=64)
+        vector_neighbours(2, "ysq_3")
         for c in range(len(CHUNKS)):
-            for t in (0, 1):
+            for t in (1, 3):
                 for side, lst in enumerate((west_sb, east_sb)):
                     nc.scalar.activation(near[t][:, side, cells[c]], logit[t][:].indirect(lst[:, entries[c]]), ACT.Sigmoid)
 
@@ -179,27 +173,35 @@ def tile_picked_fhn8_none_p_kernel(tc, x_words, x_scales, w1, rec, gn, w2, offs,
                 transpose_into(sums[b][:, t * P : (t + 1) * P], term[:, blocks[b]], start, stop)
 
         everywhere = range(len(blocks))
-        add_term(0, rec_k[0][:], everywhere, start=True)
-        add_term(1, rec_k[1][:], everywhere)
-        add_term(0, cubic[0][:], everywhere)
-        add_term(1, cubic[1][:], everywhere)
-        for t in (2, 3):
-            add_term(t, west_sum[:, t - 2, :], everywhere)
+        first_half, second_half = (0, 1), (2, 3)
+        for t in (0, 2):
+            add_term(t, rec_all[:, t, :], everywhere, start=t == 0)
+        for here in (first_half, second_half):
+            for side in range(2):
+                add_term(0, near[0][:, side, :], here)
+        for t in range(PACK):
+            if t % 2 == 1:
+                add_term(t, rec_k[t][:], everywhere)
+            add_term(t, cubic[t][:], everywhere)
+        for t in (1, 2, 3):
+            for side in range(2):
+                add_term(t, near[t][:, side, :], first_half, stop=(t, side) == (3, 1))
         back = [bank(number) for number in BACK_BANKS]
-        for c in range(2):
-            here = (2 * c, 2 * c + 1)
-            for t in (0, 1):
-                for side in range(2):
-                    add_term(t, near[t][:, side, :], here)
-            add_term(2, east_sum[:, 0, :], here)
-            add_term(3, east_sum[:, 1, :], here, stop=True)
-        for c in range(2):
-            for b in (2 * c, 2 * c + 1):
-                zt = keep.tile([P, 2, P, 2], BF16, name="zt_%d" % b, align_bytes=64)
-                nc.vector.tensor_tensor(zt[:], sums[b][:].rearrange("q (u e p) -> q u p e", u=2, e=2), gain_row[:], ALU.mult)
-                for u in range(2):
-                    start = u * CHUNKS[c] + b % 2 * P
-                    transpose_into(back[c][:, start : start + P], zt[:, u].rearrange("q p e -> q (p e)").bitcast(F32), True, True)
+
+        def apply_gain(b):
+            zt = keep.tile([P, 2, P, 2], BF16, name="zt_%d" % b, align_bytes=64)
+            nc.vector.tensor_tensor(zt[:], sums[b][:].rearrange("q (u e p) -> q u p e", u=2, e=2), gain_row[:], ALU.mult)
+            for u in range(2):
+                start = u * CHUNKS[b // 2] + b % 2 * P
+                transpose_into(back[b // 2][:, start : start + P], zt[:, u].rearrange("q p e -> q (p e)").bitcast(F32), True, True)
+
+        for side in range(2):
+            add_term(2, near[2][:, side, :], second_half)
+            add_term(1, near[1][:, side, :], second_half)
+        for side in range(2):
+            add_term(3, near[3][:, side, :], second_half, stop=side == 1)
+        for b in everywhere:
+            apply_gain(b)
         z_mx = [quantise_z(c) for c in range(2)]
         for c in range(2):
             second_product(c, *z_mx[c])

@@ -17,191 +17,195 @@ ACT = mybir.ActivationFunctionType
 K, T, S, N, H = 512, 2048, 512, 512, 512
 P = 128
 PACK = 4
-LIST_ROWS = 16
-CHUNKS = (256, 256)
-SUM_BANKS = (5, 6, 7, 0)
-BACK_BANKS = (1, 2)
-OUT_BANKS = ((3, 4, 5, 6), (7, 0, 1, 3))
-ON_VECTOR = ((1, 1), (1, 3))
+GROUP = 16
+QUADRANT = 32
+HALF = S // 2
+VECTOR_PLANES = (0, 2)
+SCALAR_PLANES = (1, 3)
 WEIGHT = (1.0, 2.0, 1.0, 2.0)
+
+GAIN_BANK = 0
+FIRST_BANKS = ((1, 7), (2,), (3,), (4,))
+SUM_BANKS = (5, 6, 7, 0)
+BACK_BANKS = (1, 2, 3, 4)
+OUT_BANKS = (SUM_BANKS, BACK_BANKS)
+
 FLOPS = 2 * K * H * S + 2 * H * N * S
 
 
 def tile_picked_fhn8_none_p_kernel(tc, x_words, x_scales, w1, rec, gn, w2, offs, west, east, out):
     nc = tc.nc
+    halves = [slice(h * HALF, (h + 1) * HALF) for h in range(2)]
+    half_entries = [slice(h * HALF // GROUP, (h + 1) * HALF // GROUP) for h in range(2)]
+    blocks = [slice(b * P, (b + 1) * P) for b in range(S // P)]
+    all_blocks, first_blocks, second_blocks = range(S // P), (0, 1), (2, 3)
+
     with ExitStack() as ctx:
         keep = ctx.enter_context(tc.tile_pool(name="keep", bufs=1))
-        head = ctx.enter_context(tc.tile_pool(name="head", bufs=1))
         psum = ctx.enter_context(tc.psum_pool(name="psum", bufs=1))
 
         def bank(number):
             return psum.tile([P, S], F32, name="bank_%d" % number)
 
-        offs_sb = keep.tile([P, S // LIST_ROWS], U16, name="offs_sb")
-        west_sb = keep.tile([P, S // LIST_ROWS], U16, name="west_sb")
-        east_sb = keep.tile([P, S // LIST_ROWS], U16, name="east_sb")
-        xw_table = head.tile([P, T], U32, name="xw_table", offset=0, align_bytes=64)
-        xs_table = keep.tile([P, T], U8, name="xs_table", tag="xs_then_w1", align_bytes=64)
+        offs_sb = keep.tile([P, S // GROUP], U16, name="offs_sb")
+        west_sb = keep.tile([P, S // GROUP], U16, name="west_sb")
+        east_sb = keep.tile([P, S // GROUP], U16, name="east_sb")
+        word_table = keep.tile([P, T], U32, name="word_table", tag="words_then_w1", align_bytes=64)
+        scale_table = keep.tile([P, T], U8, name="scale_table", align_bytes=64)
         w1_raw = keep.tile([P, PACK, H], F32, name="w1_raw", tag="w1_then_rec", align_bytes=64)
         gain = keep.tile([P, PACK], F32, name="gain")
 
-        nc.vector.memset(xs_table[:].bitcast(I32), 0)
+        nc.vector.memset(scale_table[:].bitcast(I32), 0)
         nc.sync.dma_start(gain[:], gn.rearrange("(p t) o -> p (t o)", t=PACK))
         nc.sync.dma_start(offs_sb[:], offs)
         nc.sync.dma_start(west_sb[:], west)
-        nc.sync.dma_start(xw_table[:].bitcast(I32), x_words[0].rearrange("p n t -> p (n t)").bitcast(I32))
-        for q in range(4):
-            nc.scalar.dma_start(xs_table[32 * q : 32 * q + 4, :].bitcast(I32), x_scales[0, 4 * q : 4 * q + 4, :].bitcast(I32))
         nc.sync.dma_start(w1_raw[:], w1.rearrange("(p j) c -> p j c", j=PACK))
-        w2_raw = keep.tile([P, PACK, N], F32, name="w2_raw", align_bytes=64)
-        nc.sync.dma_start(w2_raw[:], w2.rearrange("(p j) c -> p j c", j=PACK))
+        for q in range(P // QUADRANT):
+            rows = scale_table[QUADRANT * q : QUADRANT * q + 4, :]
+            nc.scalar.dma_start(rows.bitcast(I32), x_scales[0, 4 * q : 4 * q + 4, :].bitcast(I32))
+        nc.sync.dma_start(word_table[:].bitcast(I32), x_words[0].rearrange("p n t -> p (n t)").bitcast(I32))
+        w2_rows = w2.rearrange("(p j) c -> p j c", j=PACK)
+        w2_raw = [keep.tile([P, PACK, HALF], F32, name="w2_raw_%d" % h, align_bytes=64) for h in range(2)]
+        for h in range(2):
+            nc.sync.dma_start(w2_raw[h][:], w2_rows[:, :, halves[h]])
         nc.sync.dma_start(east_sb[:], east)
 
         ident = keep.tile([P, P], F32, name="ident", align_bytes=64)
         make_identity(nc, ident[:])
-        seed = keep.tile([P, 1], F32, name="seed")
-        nc.vector.memset(seed[:], 0.0)
-        warm = keep.tile([P, 1], F32, name="warm")
-        nc.scalar.activation(warm[:], seed[:], ACT.Sigmoid)
 
         def transpose_into(dst, src, start, stop):
             nc.tensor.matmul(dst, lhsT=src, rhs=ident[:], start=start, stop=stop, is_transpose=True)
 
-        gain_bank = bank(0)
-        for t in range(PACK):
-            transpose_into(gain_bank[:, t * P : (t + 1) * P], gain[:, t : t + 1].to_broadcast([P, P]), True, True)
-        gain_row = keep.tile([P, 2, P, 2], F32, name="gain_row", align_bytes=64)
-        for e in range(2):
-            planes = gain_bank[:].rearrange("q (u e p) -> q u e p", u=2, e=2)[:, :, e, :]
-            nc.scalar.activation(gain_row[:, :, :, e], planes, ACT.Copy, scale=-1.0 / WEIGHT[e])
+        zero = keep.tile([P, 1], F32, name="zero")
+        nc.vector.memset(zero[:], 0.0)
+        one_half = keep.tile([P, 1], F32, name="one_half")
+        nc.scalar.activation(one_half[:], zero[:], ACT.Sigmoid)
 
-        x_codes = keep.tile([P, S], U32, name="x_codes", align_bytes=64)
-        nc.vector.tensor_copy(x_codes[:], xw_table[:].indirect(offs_sb[:]))
-        x_scale = head.tile([P, S], U8, name="x_scale", offset=0, align_bytes=64)
-        nc.vector.tensor_copy(x_scale[:], xs_table[:].indirect(offs_sb[:]))
+        gain_bank = bank(GAIN_BANK)
+        for t in range(PACK):
+            transpose_into(gain_bank[:, blocks[t]], gain[:, t : t + 1].to_broadcast([P, P]), True, True)
+        factor = keep.tile([P, 2, P, 2], F32, name="factor", align_bytes=64)
+        for e, scale in enumerate((-1.0, one_half[:])):
+            planes = gain_bank[:].rearrange("q (u e p) -> q u e p", u=2, e=2)[:, :, e, :]
+            nc.scalar.activation(factor[:, :, :, e], planes, ACT.Copy, scale=scale)
 
         w1_cols = w1_raw[:].rearrange("p j (m t) -> p m j t", t=PACK)
-        w1_low = keep.tile([P, 2, P, PACK], BF16, name="w1_low", tag="xs_then_w1", align_bytes=64)
-        w1_high = keep.tile([P, 2, P, PACK], BF16, name="w1_high", align_bytes=64)
-        nc.vector.tensor_copy(w1_low[:].rearrange("p t m j -> p m j t"), w1_cols[:, :, :, 0:2])
-        nc.scalar.copy(w1_high[:].rearrange("p t m j -> p m j t"), w1_cols[:, :, :, 2:4])
+        w1_grouped, w1_codes, w1_scale = [], [], []
+        for pair, interleave in enumerate((nc.vector.tensor_copy, nc.scalar.copy)):
+            w1_grouped.append(keep.tile([P, 2, P, PACK], BF16, name="w1_grouped_%d" % pair, tag="w1_grouped_%d" % pair, align_bytes=64))
+            interleave(w1_grouped[pair][:].rearrange("p e m j -> p m j e"), w1_cols[:, :, :, 2 * pair : 2 * pair + 2])
 
-        rec_all = head.tile([P, PACK, S], F32, name="rec_all", offset=S, align_bytes=64)
+        def quantise_w1(pair, tag):
+            w1_codes.append(keep.tile([P, 2 * P], U32, name="w1_codes_%d" % pair, tag=tag, align_bytes=64))
+            w1_scale.append(keep.tile([P, 2 * P], U8, name="w1_scale_%d" % pair, align_bytes=64))
+            nc.vector.quantize_mx(out=w1_codes[pair][:].bitcast(FP8X4), scales=w1_scale[pair][:],
+                                  in_=w1_grouped[pair][:].rearrange("p e m j -> p (e m j)"))
+
+        quantise_w1(0, "w1_codes_0")
+        x_scale = keep.tile([P, S], U8, name="x_scale", tag="w1_grouped_0", align_bytes=64)
+        nc.vector.tensor_copy(x_scale[:], scale_table[:].indirect(offs_sb[:]))
+        x_codes = keep.tile([P, S], U32, name="x_codes", align_bytes=64)
+        for h in range(2):
+            nc.vector.tensor_copy(x_codes[:, halves[h]], word_table[:].indirect(offs_sb[:, half_entries[h]]))
+        quantise_w1(1, "words_then_w1")
+
+        rec_sb = keep.tile([P, PACK, S], F32, name="rec_sb", tag="w1_then_rec", align_bytes=64)
         rec_rows = rec.rearrange("(p t) s -> p t s", t=PACK)
-        for t in (0, 2, 1, 3):
-            nc.sync.dma_start(rec_all[:, t, :], rec_rows[:, t, :])
+        for t in VECTOR_PLANES + SCALAR_PLANES:
+            nc.sync.dma_start(rec_sb[:, t, :], rec_rows[:, t, :])
 
-        y, ysq, logit = [], [], {}
-        for pair, grouped in enumerate((w1_low, w1_high)):
-            codes = keep.tile([P, 2, P], U32, name="w1_codes_%d" % pair, tag=("w1_codes", "xs_then_w1")[pair], align_bytes=64)
-            scale = keep.tile([P, 2, P], U8, name="w1_scale_%d" % pair, align_bytes=64)
-            for e in range(2):
-                t = 2 * pair + e
-                nc.vector.quantize_mx(out=codes[:, e].bitcast(FP8X4), scales=scale[:, e], in_=grouped[:, e].rearrange("p m j -> p (m j)"))
-                acc = bank(1 + t)
-                nc.tensor.matmul_mx(out=acc[:], lhsT=codes[:, e].bitcast(FP8X4), lhsT_scale=scale[:, e],
-                                    rhs=x_codes[:].bitcast(FP8X4), rhs_scale=x_scale[:], start=True, stop=True)
-                y.append(keep.tile([P, S], F32, name="y_%d" % t, align_bytes=64))
-                ysq.append(keep.tile([P, S], F32, name="ysq_%d" % t, tag="ysq_%d" % t, align_bytes=64))
-                nc.scalar.activation(y[t][:], acc[:], ACT.Tanh)
-                nc.scalar.activation(ysq[t][:], y[t][:], ACT.Square, scale=math.sqrt(0.3125 * WEIGHT[t]))
-                if e == 1:
-                    logit[t] = keep.tile([P, S], F32, name="logit_%d" % t, align_bytes=64)
-                    nc.scalar.activation(logit[t][:], acc[:], ACT.Copy, scale=-2.0)
+        signed_y, square, logit = [], [], {}
+        for t in range(PACK):
+            signed_y.append(keep.tile([P, S], F32, name="signed_y_%d" % t, tag="signed_y_%d" % t, align_bytes=64))
+            square.append(keep.tile([P, S], F32, name="square_%d" % t, tag="square_%d" % t, align_bytes=64))
+            width = S // len(FIRST_BANKS[t])
+            for part, number in enumerate(FIRST_BANKS[t]):
+                cols = slice(part * width, (part + 1) * width)
+                acc = bank(number)
+                nc.tensor.matmul_mx(out=acc[:, cols], lhsT=w1_codes[t // 2][:, blocks[t % 2]].bitcast(FP8X4), lhsT_scale=w1_scale[t // 2][:, blocks[t % 2]],
+                                    rhs=x_codes[:, cols].bitcast(FP8X4), rhs_scale=x_scale[:, cols], start=True, stop=True)
+                nc.scalar.activation(signed_y[t][:, cols], acc[:, cols], ACT.Tanh, scale=-1.0 if t in SCALAR_PLANES else 1.0)
+            nc.scalar.activation(square[t][:], signed_y[t][:], ACT.Square, scale=math.sqrt(0.3125 * WEIGHT[t]))
+            if t in SCALAR_PLANES:
+                logit[t] = keep.tile([P, S], F32, name="logit_%d" % t, align_bytes=64)
+                nc.scalar.activation(logit[t][:], acc[:], ACT.Copy, scale=2.0)
 
-        w2_codes = keep.tile([P, N], U32, name="w2_codes", align_bytes=64)
-        w2_scale = keep.tile([P, N], U8, name="w2_scale", align_bytes=64)
         w2_grouped = keep.tile([P, N, PACK], BF16, name="w2_grouped", align_bytes=64)
-        nc.vector.tensor_copy(w2_grouped[:].rearrange("p (c i) j -> p c j i", i=4), w2_raw[:].rearrange("p j (c i) -> p c j i", i=4))
-        nc.vector.quantize_mx(out=w2_codes[:].bitcast(FP8X4), scales=w2_scale[:], in_=w2_grouped[:].rearrange("p c j -> p (c j)"))
+        for h in range(2):
+            nc.vector.tensor_copy(w2_grouped[:, halves[h], :].rearrange("p (c i) j -> p c j i", i=4),
+                                  w2_raw[h][:].rearrange("p j (c i) -> p c j i", i=4))
 
-        firsts = [sum(CHUNKS[:c]) for c in range(len(CHUNKS))]
-        cells = [slice(first, first + width) for first, width in zip(firsts, CHUNKS)]
-        entries = [slice(first // LIST_ROWS, (first + width) // LIST_ROWS) for first, width in zip(firsts, CHUNKS)]
-        halves = (slice(0, S // 2), slice(S // 2, S))
-        blocks = [slice(b * P, (b + 1) * P) for b in range(S // P)]
-
-        rec_k, cubic, near = {}, [], {}
+        rec_term, cubic, near = {}, [], {}
 
         def vector_neighbours(t, tag):
             near[t] = keep.tile([P, 2, S], F32, name="near_%d" % t, tag=tag, align_bytes=64)
-            for c in range(len(CHUNKS)):
-                for side, lst in enumerate((west_sb, east_sb)):
-                    nc.vector.tensor_scalar(near[t][:, side, cells[c]], y[t][:].indirect(lst[:, entries[c]]), -0.25, 0.0, ALU.mult, ALU.add)
+            for h in range(2):
+                for side, places in enumerate((west_sb, east_sb)):
+                    window = signed_y[t][:].indirect(places[:, half_entries[h]])
+                    nc.vector.tensor_scalar(near[t][:, side, halves[h]], window, -0.25, 0.0, ALU.mult, ALU.add)
 
         vector_neighbours(0, "near_0")
         for t in range(PACK):
-            if t % 2 == 1:
+            if t in SCALAR_PLANES:
                 near[t] = keep.tile([P, 2, S], F32, name="near_%d" % t, align_bytes=64)
-                rec_k[t] = keep.tile([P, S], F32, name="rec_k_%d" % t, align_bytes=64)
-                nc.vector.tensor_scalar(rec_k[t][:], rec_all[:, t, :], 2.0, -1.0, ALU.mult, ALU.add)
+                rec_term[t] = keep.tile([P, S], F32, name="rec_term_%d" % t, align_bytes=64)
+                nc.vector.tensor_scalar(rec_term[t][:], rec_sb[:, t, :], -2.0, -1.0, ALU.mult, ALU.add)
             cubic.append(keep.tile([P, S], F32, name="cubic_%d" % t, align_bytes=64))
-            nc.vector.scalar_tensor_tensor(cubic[t][:], ysq[t][:], WEIGHT[t], y[t][:], ALU.subtract, ALU.mult)
-        vector_neighbours(2, "ysq_3")
-        for c in range(len(CHUNKS)):
-            for t in (1, 3):
-                for side, lst in enumerate((west_sb, east_sb)):
-                    nc.scalar.activation(near[t][:, side, cells[c]], logit[t][:].indirect(lst[:, entries[c]]), ACT.Sigmoid)
-
-        def quantise_z(c):
-            width = CHUNKS[c]
-            z16 = keep.tile([P, width * PACK], BF16, name="z16_%d" % c, align_bytes=64)
-            nc.scalar.copy(z16[:].bitcast(F32).rearrange("p (n u) -> p n u", u=2), back[c][:, 0 : 2 * width].rearrange("p (u n) -> p n u", u=2))
-            z_codes = keep.tile([P, width], U32, name="z_codes_%d" % c, align_bytes=64)
-            z_scale = keep.tile([P, width], U8, name="z_scale_%d" % c, align_bytes=64)
-            nc.vector.quantize_mx(out=z_codes[:].bitcast(FP8X4), scales=z_scale[:], in_=z16[:])
-            return z_codes, z_scale
-
-        def second_product(c, z_codes, z_scale):
-            width = CHUNKS[c]
-            per_bank = N // P // len(OUT_BANKS[c])
-            for b, number in enumerate(OUT_BANKS[c]):
-                acc = bank(number)
-                for a in range(per_bank):
-                    cols = slice((per_bank * b + a) * P, (per_bank * b + a + 1) * P)
-                    nc.tensor.matmul_mx(out=acc[:, a * width : (a + 1) * width], lhsT=w2_codes[:, cols].bitcast(FP8X4), lhsT_scale=w2_scale[:, cols],
-                                        rhs=z_codes[:].bitcast(FP8X4), rhs_scale=z_scale[:], start=True, stop=True)
-                result = keep.tile([P, per_bank, width], F32, name="result_%d_%d" % (c, b), align_bytes=64)
-                evacuate = nc.vector.tensor_copy if (c, b) in ON_VECTOR else nc.scalar.copy
-                evacuate(result[:].rearrange("p a n -> p (a n)"), acc[:, 0 : per_bank * width])
-                nc.sync.dma_start(out[per_bank * b * P : per_bank * (b + 1) * P, cells[c]].rearrange("(a p) n -> p a n", p=P), result[:])
+            nc.vector.scalar_tensor_tensor(cubic[t][:], square[t][:], WEIGHT[t], signed_y[t][:], ALU.subtract, ALU.mult)
+        vector_neighbours(2, "square_3")
+        w2_codes = keep.tile([P, N], U32, name="w2_codes", tag="signed_y_2", align_bytes=64)
+        w2_scale = keep.tile([P, N], U8, name="w2_scale", align_bytes=64)
+        nc.vector.quantize_mx(out=w2_codes[:].bitcast(FP8X4), scales=w2_scale[:], in_=w2_grouped[:].rearrange("p c j -> p (c j)"))
+        for h in range(2):
+            for t in SCALAR_PLANES:
+                for side, places in enumerate((west_sb, east_sb)):
+                    nc.scalar.activation(near[t][:, side, halves[h]], logit[t][:].indirect(places[:, half_entries[h]]), ACT.Sigmoid)
 
         sums = [bank(number) for number in SUM_BANKS]
 
         def add_term(t, term, where, start=False, stop=False):
             for b in where:
-                transpose_into(sums[b][:, t * P : (t + 1) * P], term[:, blocks[b]], start, stop)
+                transpose_into(sums[b][:, blocks[t]], term[:, blocks[b]], start, stop)
 
-        everywhere = range(len(blocks))
-        first_half, second_half = (0, 1), (2, 3)
-        for t in (0, 2):
-            add_term(t, rec_all[:, t, :], everywhere, start=t == 0)
-        for here in (first_half, second_half):
+        for t in VECTOR_PLANES:
+            add_term(t, rec_sb[:, t, :], all_blocks, start=t == 0)
+        for where in (first_blocks, second_blocks):
             for side in range(2):
-                add_term(0, near[0][:, side, :], here)
+                add_term(0, near[0][:, side, :], where)
         for t in range(PACK):
-            if t % 2 == 1:
-                add_term(t, rec_k[t][:], everywhere)
-            add_term(t, cubic[t][:], everywhere)
+            if t in SCALAR_PLANES:
+                add_term(t, rec_term[t][:], all_blocks)
+            add_term(t, cubic[t][:], all_blocks)
         for t in (1, 2, 3):
             for side in range(2):
-                add_term(t, near[t][:, side, :], first_half, stop=(t, side) == (3, 1))
+                add_term(t, near[t][:, side, :], first_blocks, stop=(t, side) == (3, 1))
+        for side in range(2):
+            for t in (2, 1):
+                add_term(t, near[t][:, side, :], second_blocks)
+        for side in range(2):
+            add_term(3, near[3][:, side, :], second_blocks, stop=side == 1)
+
         back = [bank(number) for number in BACK_BANKS]
-
-        def apply_gain(b):
-            zt = keep.tile([P, 2, P, 2], BF16, name="zt_%d" % b, align_bytes=64)
-            nc.vector.tensor_tensor(zt[:], sums[b][:].rearrange("q (u e p) -> q u p e", u=2, e=2), gain_row[:], ALU.mult)
+        for b in all_blocks:
+            z_turned = keep.tile([P, 2, P, 2], BF16, name="z_turned_%d" % b, align_bytes=64)
+            nc.vector.tensor_tensor(z_turned[:], sums[b][:].rearrange("q (u e p) -> q u p e", u=2, e=2), factor[:], ALU.mult)
             for u in range(2):
-                start = u * CHUNKS[b // 2] + b % 2 * P
-                transpose_into(back[b // 2][:, start : start + P], zt[:, u].rearrange("q p e -> q (p e)").bitcast(F32), True, True)
+                transpose_into(back[b][:, blocks[u]], z_turned[:, u].rearrange("q p e -> q (p e)").bitcast(F32), True, True)
 
-        for side in range(2):
-            add_term(2, near[2][:, side, :], second_half)
-            add_term(1, near[1][:, side, :], second_half)
-        for side in range(2):
-            add_term(3, near[3][:, side, :], second_half, stop=side == 1)
-        for b in everywhere:
-            apply_gain(b)
-        z_mx = [quantise_z(c) for c in range(2)]
-        for c in range(2):
-            second_product(c, *z_mx[c])
+        z_codes = keep.tile([P, S], U32, name="z_codes", align_bytes=64)
+        z_scale = keep.tile([P, S], U8, name="z_scale", align_bytes=64)
+        for b in all_blocks:
+            z_grouped = keep.tile([P, P * PACK], BF16, name="z_grouped_%d" % b, align_bytes=64)
+            nc.scalar.copy(z_grouped[:].bitcast(F32).rearrange("p (c u) -> p c u", u=2),
+                           back[b][:, 0 : 2 * P].rearrange("p (u c) -> p c u", u=2))
+            nc.vector.quantize_mx(out=z_codes[:, blocks[b]].bitcast(FP8X4), scales=z_scale[:, blocks[b]], in_=z_grouped[:])
+
+        for h in range(2):
+            for m, number in enumerate(OUT_BANKS[h]):
+                acc = bank(number)
+                nc.tensor.matmul_mx(out=acc[:, 0:HALF], lhsT=w2_codes[:, blocks[m]].bitcast(FP8X4), lhsT_scale=w2_scale[:, blocks[m]],
+                                    rhs=z_codes[:, halves[h]].bitcast(FP8X4), rhs_scale=z_scale[:, halves[h]], start=True, stop=True)
+                result = keep.tile([P, HALF], F32, name="result_%d_%d" % (h, m), align_bytes=64)
+                empty = nc.vector.tensor_copy if (h == 1 and m % 2 == 1) else nc.scalar.copy
+                empty(result[:], acc[:, 0:HALF])
+                nc.sync.dma_start(out[blocks[m], halves[h]], result[:])

@@ -56,19 +56,18 @@ def tile_picked_fhn8_none_p_kernel(tc, x_words, x_scales, w1, rec, gn, w2, offs,
         gain = keep.tile([P, PACK], F32, name="gain")
 
         nc.vector.memset(scale_table[:].bitcast(I32), 0)
-        nc.sync.dma_start(gain[:], gn.rearrange("(p t) o -> p (t o)", t=PACK))
-        nc.sync.dma_start(offs_sb[:], offs)
-        nc.sync.dma_start(west_sb[:], west)
+        nc.scalar.dma_start(gain[:], gn.rearrange("(p t) o -> p (t o)", t=PACK))
         nc.sync.dma_start(w1_raw[:], w1.rearrange("(p j) c -> p j c", j=PACK))
-        for q in range(P // QUADRANT):
-            rows = scale_table[QUADRANT * q : QUADRANT * q + 4, :]
-            nc.scalar.dma_start(rows.bitcast(I32), x_scales[0, 4 * q : 4 * q + 4, :].bitcast(I32))
+        nc.sync.dma_start(offs_sb[:], offs)
+        for r in range(4):
+            nc.sync.dma_start(scale_table[r:P:QUADRANT, :].bitcast(I32), x_scales[0, r:16:4, :].bitcast(I32))
         nc.sync.dma_start(word_table[:].bitcast(I32), x_words[0].rearrange("p n t -> p (n t)").bitcast(I32))
         w2_rows = w2.rearrange("(p j) c -> p j c", j=PACK)
         w2_raw = [keep.tile([P, PACK, HALF], F32, name="w2_raw_%d" % h, align_bytes=64) for h in range(2)]
-        for h in range(2):
-            nc.sync.dma_start(w2_raw[h][:], w2_rows[:, :, halves[h]])
+        nc.sync.dma_start(w2_raw[0][:], w2_rows[:, :, halves[0]])
+        nc.sync.dma_start(west_sb[:], west)
         nc.sync.dma_start(east_sb[:], east)
+        nc.sync.dma_start(w2_raw[1][:], w2_rows[:, :, halves[1]])
 
         ident = keep.tile([P, P], F32, name="ident", align_bytes=64)
         make_identity(nc, ident[:])
@@ -80,12 +79,15 @@ def tile_picked_fhn8_none_p_kernel(tc, x_words, x_scales, w1, rec, gn, w2, offs,
         nc.vector.memset(zero[:], 0.0)
         one_half = keep.tile([P, 1], F32, name="one_half")
         nc.scalar.activation(one_half[:], zero[:], ACT.Sigmoid)
+        minus_half = keep.tile([P, 1], F32, name="minus_half")
+        nc.scalar.activation(minus_half[:], one_half[:], ACT.Copy, scale=-1.0)
 
         gain_bank = bank(GAIN_BANK)
         for t in range(PACK):
             transpose_into(gain_bank[:, blocks[t]], gain[:, t : t + 1].to_broadcast([P, P]), True, True)
-        factor = keep.tile([P, 2, P, 2], F32, name="factor", align_bytes=64)
-        for e, scale in enumerate((-1.0, one_half[:])):
+        window_0 = keep.tile([P, 2 * S], F32, name="window_0", align_bytes=64)
+        factor = window_0[:, S : 2 * S].rearrange("q (u p e) -> q u p e", u=2, e=2)
+        for e, scale in enumerate((-1.0, minus_half[:])):
             planes = gain_bank[:].rearrange("q (u e p) -> q u e p", u=2, e=2)[:, :, e, :]
             nc.scalar.activation(factor[:, :, :, e], planes, ACT.Copy, scale=scale)
 
@@ -116,7 +118,7 @@ def tile_picked_fhn8_none_p_kernel(tc, x_words, x_scales, w1, rec, gn, w2, offs,
 
         signed_y, square, logit = [], [], {}
         for t in range(PACK):
-            signed_y.append(keep.tile([P, S], F32, name="signed_y_%d" % t, tag="signed_y_%d" % t, align_bytes=64))
+            signed_y.append(keep.tile([P, S], F32, name="signed_y_%d" % t, tag="signed_y_%d" % t, align_bytes=64) if t > 0 else window_0[:, 0:S])
             square.append(keep.tile([P, S], F32, name="square_%d" % t, tag="square_%d" % t, align_bytes=64))
             width = S // len(FIRST_BANKS[t])
             for part, number in enumerate(FIRST_BANKS[t]):
@@ -124,32 +126,34 @@ def tile_picked_fhn8_none_p_kernel(tc, x_words, x_scales, w1, rec, gn, w2, offs,
                 acc = bank(number)
                 nc.tensor.matmul_mx(out=acc[:, cols], lhsT=w1_codes[t // 2][:, blocks[t % 2]].bitcast(FP8X4), lhsT_scale=w1_scale[t // 2][:, blocks[t % 2]],
                                     rhs=x_codes[:, cols].bitcast(FP8X4), rhs_scale=x_scale[:, cols], start=True, stop=True)
-                nc.scalar.activation(signed_y[t][:, cols], acc[:, cols], ACT.Tanh, scale=-1.0 if t in SCALAR_PLANES else 1.0)
-            nc.scalar.activation(square[t][:], signed_y[t][:], ACT.Square, scale=math.sqrt(0.3125 * WEIGHT[t]))
+                nc.scalar.activation(signed_y[t][:, cols], acc[:, cols], ACT.Tanh)
+            if t > 0:
+                nc.scalar.activation(square[t][:], signed_y[t][:], ACT.Square, scale=math.sqrt(0.3125 * WEIGHT[t]))
             if t in SCALAR_PLANES:
                 logit[t] = keep.tile([P, S], F32, name="logit_%d" % t, align_bytes=64)
-                nc.scalar.activation(logit[t][:], acc[:], ACT.Copy, scale=2.0)
+                nc.scalar.activation(logit[t][:], acc[:], ACT.Copy, scale=-2.0)
 
         w2_grouped = keep.tile([P, N, PACK], BF16, name="w2_grouped", align_bytes=64)
         for h in range(2):
             nc.vector.tensor_copy(w2_grouped[:, halves[h], :].rearrange("p (c i) j -> p c j i", i=4),
                                   w2_raw[h][:].rearrange("p j (c i) -> p c j i", i=4))
 
-        rec_term, cubic, near = {}, [], {}
+        cubic, near = [], {}
 
         def vector_neighbours(t, tag):
             near[t] = keep.tile([P, 2, S], F32, name="near_%d" % t, tag=tag, align_bytes=64)
             for h in range(2):
                 for side, places in enumerate((west_sb, east_sb)):
                     window = signed_y[t][:].indirect(places[:, half_entries[h]])
-                    nc.vector.tensor_scalar(near[t][:, side, halves[h]], window, -0.25, 0.0, ALU.mult, ALU.add)
+                    nc.vector.tensor_scalar(near[t][:, side, halves[h]], window, -0.25, 0.5, ALU.mult, ALU.add)
 
-        vector_neighbours(0, "near_0")
+        nc.vector.scalar_tensor_tensor(square[0][:], signed_y[0][:], 0.3125, signed_y[0][:], ALU.mult, ALU.mult)
+        near[0] = keep.tile([P, 2, S], F32, name="near_0", align_bytes=64)
+        for side, places in enumerate((west_sb, east_sb)):
+            nc.vector.tensor_scalar(near[0][:, side, :], window_0[:].indirect(places[:]), -0.25, 0.5, ALU.mult, ALU.add)
         for t in range(PACK):
             if t in SCALAR_PLANES:
                 near[t] = keep.tile([P, 2, S], F32, name="near_%d" % t, align_bytes=64)
-                rec_term[t] = keep.tile([P, S], F32, name="rec_term_%d" % t, align_bytes=64)
-                nc.vector.tensor_scalar(rec_term[t][:], rec_sb[:, t, :], -2.0, -1.0, ALU.mult, ALU.add)
             cubic.append(keep.tile([P, S], F32, name="cubic_%d" % t, align_bytes=64))
             nc.vector.scalar_tensor_tensor(cubic[t][:], square[t][:], WEIGHT[t], signed_y[t][:], ALU.subtract, ALU.mult)
         vector_neighbours(2, "square_3")
@@ -165,7 +169,7 @@ def tile_picked_fhn8_none_p_kernel(tc, x_words, x_scales, w1, rec, gn, w2, offs,
 
         def add_term(t, term, where, start=False, stop=False):
             for b in where:
-                transpose_into(sums[b][:, blocks[t]], term[:, blocks[b]], start, stop)
+                transpose_into(sums[b][:, blocks[2 * (t % 2) + t // 2]], term[:, blocks[b]], start, stop)
 
         for t in VECTOR_PLANES:
             add_term(t, rec_sb[:, t, :], all_blocks, start=t == 0)
@@ -174,7 +178,8 @@ def tile_picked_fhn8_none_p_kernel(tc, x_words, x_scales, w1, rec, gn, w2, offs,
                 add_term(0, near[0][:, side, :], where)
         for t in range(PACK):
             if t in SCALAR_PLANES:
-                add_term(t, rec_term[t][:], all_blocks)
+                for turn in range(2):
+                    add_term(t, rec_sb[:, t, :], all_blocks)
             add_term(t, cubic[t][:], all_blocks)
         for t in (1, 2, 3):
             for side in range(2):
@@ -188,7 +193,8 @@ def tile_picked_fhn8_none_p_kernel(tc, x_words, x_scales, w1, rec, gn, w2, offs,
         back = [bank(number) for number in BACK_BANKS]
         for b in all_blocks:
             z_turned = keep.tile([P, 2, P, 2], BF16, name="z_turned_%d" % b, align_bytes=64)
-            nc.vector.tensor_tensor(z_turned[:], sums[b][:].rearrange("q (u e p) -> q u p e", u=2, e=2), factor[:], ALU.mult)
+            nc.vector.scalar_tensor_tensor(z_turned[:].rearrange("q u p e -> q (u p) e"), sums[b][:].rearrange("q (e c) -> q c e", e=2), 1.0,
+                                           window_0[:, S : 2 * S].rearrange("q (c e) -> q c e", e=2), ALU.subtract, ALU.mult)
             for u in range(2):
                 transpose_into(back[b][:, blocks[u]], z_turned[:, u].rearrange("q p e -> q (p e)").bitcast(F32), True, True)
 
@@ -200,12 +206,15 @@ def tile_picked_fhn8_none_p_kernel(tc, x_words, x_scales, w1, rec, gn, w2, offs,
                            back[b][:, 0 : 2 * P].rearrange("p (u c) -> p c u", u=2))
             nc.vector.quantize_mx(out=z_codes[:, blocks[b]].bitcast(FP8X4), scales=z_scale[:, blocks[b]], in_=z_grouped[:])
 
-        for h in range(2):
-            for m, number in enumerate(OUT_BANKS[h]):
-                acc = bank(number)
-                nc.tensor.matmul_mx(out=acc[:, 0:HALF], lhsT=w2_codes[:, blocks[m]].bitcast(FP8X4), lhsT_scale=w2_scale[:, blocks[m]],
-                                    rhs=z_codes[:, halves[h]].bitcast(FP8X4), rhs_scale=z_scale[:, halves[h]], start=True, stop=True)
+        for h, parts in enumerate(((halves[0],), (blocks[2], blocks[3]))):
+            accs = [bank(number) for number in OUT_BANKS[h]]
+            for cells in parts:
+                for m in range(PACK):
+                    place = slice(cells.start - halves[h].start, cells.stop - halves[h].start)
+                    nc.tensor.matmul_mx(out=accs[m][:, place], lhsT=w2_codes[:, blocks[m]].bitcast(FP8X4), lhsT_scale=w2_scale[:, blocks[m]],
+                                        rhs=z_codes[:, cells].bitcast(FP8X4), rhs_scale=z_scale[:, cells], start=True, stop=True)
+            for m in range(PACK):
                 result = keep.tile([P, HALF], F32, name="result_%d_%d" % (h, m), align_bytes=64)
                 empty = nc.vector.tensor_copy if (h == 1 and m % 2 == 1) else nc.scalar.copy
-                empty(result[:], acc[:, 0:HALF])
+                empty(result[:], accs[m][:, 0:HALF])
                 nc.sync.dma_start(out[blocks[m], halves[h]], result[:])

@@ -127,8 +127,8 @@ def tile_picked_fhn8_none_p_kernel(tc, x_words, x_scales, w1, rec, gn, w2, offs,
                 nc.tensor.matmul_mx(out=acc[:, cols], lhsT=w1_codes[t // 2][:, blocks[t % 2]].bitcast(FP8X4), lhsT_scale=w1_scale[t // 2][:, blocks[t % 2]],
                                     rhs=x_codes[:, cols].bitcast(FP8X4), rhs_scale=x_scale[:, cols], start=True, stop=True)
                 nc.scalar.activation(signed_y[t][:, cols], acc[:, cols], ACT.Tanh)
-            if t > 0:
-                nc.scalar.activation(square[t][:], signed_y[t][:], ACT.Square, scale=math.sqrt(0.3125 * WEIGHT[t]))
+            cells = slice(0, S) if t > 0 else halves[1]
+            nc.scalar.activation(square[t][:, cells], signed_y[t][:, cells], ACT.Square, scale=math.sqrt(0.3125 * WEIGHT[t]))
             if t in SCALAR_PLANES:
                 logit[t] = keep.tile([P, S], F32, name="logit_%d" % t, align_bytes=64)
                 nc.scalar.activation(logit[t][:], acc[:], ACT.Copy, scale=-2.0)
@@ -147,7 +147,7 @@ def tile_picked_fhn8_none_p_kernel(tc, x_words, x_scales, w1, rec, gn, w2, offs,
                     window = signed_y[t][:].indirect(places[:, half_entries[h]])
                     nc.vector.tensor_scalar(near[t][:, side, halves[h]], window, -0.25, 0.5, ALU.mult, ALU.add)
 
-        nc.vector.scalar_tensor_tensor(square[0][:], signed_y[0][:], 0.3125, signed_y[0][:], ALU.mult, ALU.mult)
+        nc.vector.scalar_tensor_tensor(square[0][:, halves[0]], signed_y[0][:, halves[0]], 0.3125, signed_y[0][:, halves[0]], ALU.mult, ALU.mult)
         near[0] = keep.tile([P, 2, S], F32, name="near_0", align_bytes=64)
         for side, places in enumerate((west_sb, east_sb)):
             nc.vector.tensor_scalar(near[0][:, side, :], window_0[:].indirect(places[:]), -0.25, 0.5, ALU.mult, ALU.add)
@@ -160,10 +160,10 @@ def tile_picked_fhn8_none_p_kernel(tc, x_words, x_scales, w1, rec, gn, w2, offs,
         w2_codes = keep.tile([P, N], U32, name="w2_codes", tag="signed_y_2", align_bytes=64)
         w2_scale = keep.tile([P, N], U8, name="w2_scale", align_bytes=64)
         nc.vector.quantize_mx(out=w2_codes[:].bitcast(FP8X4), scales=w2_scale[:], in_=w2_grouped[:].rearrange("p c j -> p (c j)"))
-        for h in range(2):
-            for t in SCALAR_PLANES:
-                for side, places in enumerate((west_sb, east_sb)):
-                    nc.scalar.activation(near[t][:, side, halves[h]], logit[t][:].indirect(places[:, half_entries[h]]), ACT.Sigmoid)
+        for t, cells in ((1, halves[0]), (3, halves[0]), (1, halves[1]), (3, blocks[2]), (3, blocks[3])):
+            for side, places in enumerate((west_sb, east_sb)):
+                entries = slice(cells.start // GROUP, cells.stop // GROUP)
+                nc.scalar.activation(near[t][:, side, cells], logit[t][:].indirect(places[:, entries]), ACT.Sigmoid)
 
         sums = [bank(number) for number in SUM_BANKS]
 
@@ -176,10 +176,10 @@ def tile_picked_fhn8_none_p_kernel(tc, x_words, x_scales, w1, rec, gn, w2, offs,
         for where in (first_blocks, second_blocks):
             for side in range(2):
                 add_term(0, near[0][:, side, :], where)
+        for t in SCALAR_PLANES:
+            for turn in range(2):
+                add_term(t, rec_sb[:, t, :], all_blocks)
         for t in range(PACK):
-            if t in SCALAR_PLANES:
-                for turn in range(2):
-                    add_term(t, rec_sb[:, t, :], all_blocks)
             add_term(t, cubic[t][:], all_blocks)
         for t in (1, 2, 3):
             for side in range(2):
@@ -187,8 +187,9 @@ def tile_picked_fhn8_none_p_kernel(tc, x_words, x_scales, w1, rec, gn, w2, offs,
         for side in range(2):
             for t in (2, 1):
                 add_term(t, near[t][:, side, :], second_blocks)
-        for side in range(2):
-            add_term(3, near[3][:, side, :], second_blocks, stop=side == 1)
+        for b in second_blocks:
+            for side in range(2):
+                add_term(3, near[3][:, side, :], (b,), stop=side == 1)
 
         back = [bank(number) for number in BACK_BANKS]
         for b in all_blocks:
@@ -217,4 +218,5 @@ def tile_picked_fhn8_none_p_kernel(tc, x_words, x_scales, w1, rec, gn, w2, offs,
                 result = keep.tile([P, HALF], F32, name="result_%d_%d" % (h, m), align_bytes=64)
                 empty = nc.vector.tensor_copy if (h == 1 and m % 2 == 1) else nc.scalar.copy
                 empty(result[:], accs[m][:, 0:HALF])
-                nc.sync.dma_start(out[blocks[m], halves[h]], result[:])
+                queue = nc.scalar if (h, m) == (1, 2) else nc.sync
+                queue.dma_start(out[blocks[m], halves[h]], result[:])

@@ -22,7 +22,6 @@ QUADRANT = 32
 HALF = S // 2
 VECTOR_PLANES = (0, 2)
 SCALAR_PLANES = (1, 3)
-WEIGHT = (1.0, 2.0, 1.0, 2.0)
 
 GAIN_BANK = 0
 FIRST_BANKS = ((1, 7), (2,), (3,), (4,))
@@ -75,21 +74,12 @@ def tile_picked_fhn8_none_p_kernel(tc, x_words, x_scales, w1, rec, gn, w2, offs,
         def transpose_into(dst, src, start, stop):
             nc.tensor.matmul(dst, lhsT=src, rhs=ident[:], start=start, stop=stop, is_transpose=True)
 
-        zero = keep.tile([P, 1], F32, name="zero")
-        nc.vector.memset(zero[:], 0.0)
-        one_half = keep.tile([P, 1], F32, name="one_half")
-        nc.scalar.activation(one_half[:], zero[:], ACT.Sigmoid)
-        minus_half = keep.tile([P, 1], F32, name="minus_half")
-        nc.scalar.activation(minus_half[:], one_half[:], ACT.Copy, scale=-1.0)
-
         gain_bank = bank(GAIN_BANK)
         for t in range(PACK):
             transpose_into(gain_bank[:, blocks[t]], gain[:, t : t + 1].to_broadcast([P, P]), True, True)
         window_0 = keep.tile([P, 2 * S], F32, name="window_0", align_bytes=64)
         factor = window_0[:, S : 2 * S].rearrange("q (u p e) -> q u p e", u=2, e=2)
-        for e, scale in enumerate((-1.0, minus_half[:])):
-            planes = gain_bank[:].rearrange("q (u e p) -> q u e p", u=2, e=2)[:, :, e, :]
-            nc.scalar.activation(factor[:, :, :, e], planes, ACT.Copy, scale=scale)
+        nc.scalar.activation(factor, gain_bank[:].rearrange("q (u e p) -> q u p e", u=2, e=2), ACT.Copy, scale=-1.0)
 
         w1_cols = w1_raw[:].rearrange("p j (m t) -> p m j t", t=PACK)
         w1_grouped, w1_codes, w1_scale = [], [], []
@@ -116,7 +106,7 @@ def tile_picked_fhn8_none_p_kernel(tc, x_words, x_scales, w1, rec, gn, w2, offs,
         for t in VECTOR_PLANES + SCALAR_PLANES:
             nc.sync.dma_start(rec_sb[:, t, :], rec_rows[:, t, :])
 
-        signed_y, square, logit = [], [], {}
+        signed_y, square = [], []
         for t in range(PACK):
             signed_y.append(keep.tile([P, S], F32, name="signed_y_%d" % t, tag="signed_y_%d" % t, align_bytes=64) if t > 0 else window_0[:, 0:S])
             square.append(keep.tile([P, S], F32, name="square_%d" % t, tag="square_%d" % t, align_bytes=64))
@@ -127,11 +117,7 @@ def tile_picked_fhn8_none_p_kernel(tc, x_words, x_scales, w1, rec, gn, w2, offs,
                 nc.tensor.matmul_mx(out=acc[:, cols], lhsT=w1_codes[t // 2][:, blocks[t % 2]].bitcast(FP8X4), lhsT_scale=w1_scale[t // 2][:, blocks[t % 2]],
                                     rhs=x_codes[:, cols].bitcast(FP8X4), rhs_scale=x_scale[:, cols], start=True, stop=True)
                 nc.scalar.activation(signed_y[t][:, cols], acc[:, cols], ACT.Tanh)
-            cells = slice(0, S) if t > 0 else halves[1]
-            nc.scalar.activation(square[t][:, cells], signed_y[t][:, cells], ACT.Square, scale=math.sqrt(0.3125 * WEIGHT[t]))
-            if t in SCALAR_PLANES:
-                logit[t] = keep.tile([P, S], F32, name="logit_%d" % t, align_bytes=64)
-                nc.scalar.activation(logit[t][:], acc[:], ACT.Copy, scale=-2.0)
+            nc.scalar.activation(square[t][:], signed_y[t][:], ACT.Square, scale=math.sqrt(0.3125))
 
         w2_grouped = keep.tile([P, N, PACK], BF16, name="w2_grouped", align_bytes=64)
         for h in range(2):
@@ -144,26 +130,28 @@ def tile_picked_fhn8_none_p_kernel(tc, x_words, x_scales, w1, rec, gn, w2, offs,
             near[t] = keep.tile([P, 2, S], F32, name="near_%d" % t, tag=tag, align_bytes=64)
             for h in range(2):
                 for side, places in enumerate((west_sb, east_sb)):
-                    window = signed_y[t][:].indirect(places[:, half_entries[h]])
-                    nc.vector.tensor_scalar(near[t][:, side, halves[h]], window, -0.25, 0.5, ALU.mult, ALU.add)
+                    cells = blocks[2] if (h, side) == (1, 1) else halves[h]
+                    window = signed_y[t][:].indirect(places[:, cells.start // GROUP : cells.stop // GROUP])
+                    nc.vector.tensor_scalar(near[t][:, side, cells], window, -0.25, 0.0, ALU.mult, ALU.add)
 
-        nc.vector.scalar_tensor_tensor(square[0][:, halves[0]], signed_y[0][:, halves[0]], 0.3125, signed_y[0][:, halves[0]], ALU.mult, ALU.mult)
         near[0] = keep.tile([P, 2, S], F32, name="near_0", align_bytes=64)
         for side, places in enumerate((west_sb, east_sb)):
-            nc.vector.tensor_scalar(near[0][:, side, :], window_0[:].indirect(places[:]), -0.25, 0.5, ALU.mult, ALU.add)
+            nc.vector.tensor_scalar(near[0][:, side, :], window_0[:].indirect(places[:]), -0.25, 0.0, ALU.mult, ALU.add)
         for t in range(PACK):
             if t in SCALAR_PLANES:
                 near[t] = keep.tile([P, 2, S], F32, name="near_%d" % t, align_bytes=64)
             cubic.append(keep.tile([P, S], F32, name="cubic_%d" % t, align_bytes=64))
-            nc.vector.scalar_tensor_tensor(cubic[t][:], square[t][:], WEIGHT[t], signed_y[t][:], ALU.subtract, ALU.mult)
+            nc.vector.scalar_tensor_tensor(cubic[t][:], square[t][:], 1.0, signed_y[t][:], ALU.subtract, ALU.mult)
         vector_neighbours(2, "square_3")
+        spare = keep.tile([P, P], F32, name="spare", align_bytes=64)
+        nc.scalar.activation(spare[:], signed_y[2][:].indirect(east_sb[:, blocks[3].start // GROUP : blocks[3].stop // GROUP]), ACT.Copy, scale=-0.25)
         w2_codes = keep.tile([P, N], U32, name="w2_codes", tag="signed_y_2", align_bytes=64)
         w2_scale = keep.tile([P, N], U8, name="w2_scale", align_bytes=64)
         nc.vector.quantize_mx(out=w2_codes[:].bitcast(FP8X4), scales=w2_scale[:], in_=w2_grouped[:].rearrange("p c j -> p (c j)"))
         for t, cells in ((1, halves[0]), (3, halves[0]), (1, halves[1]), (3, blocks[2]), (3, blocks[3])):
             for side, places in enumerate((west_sb, east_sb)):
                 entries = slice(cells.start // GROUP, cells.stop // GROUP)
-                nc.scalar.activation(near[t][:, side, cells], logit[t][:].indirect(places[:, entries]), ACT.Sigmoid)
+                nc.scalar.activation(near[t][:, side, cells], signed_y[t][:].indirect(places[:, entries]), ACT.Copy, scale=-0.25)
 
         sums = [bank(number) for number in SUM_BANKS]
 
@@ -177,16 +165,16 @@ def tile_picked_fhn8_none_p_kernel(tc, x_words, x_scales, w1, rec, gn, w2, offs,
             for side in range(2):
                 add_term(0, near[0][:, side, :], where)
         for t in SCALAR_PLANES:
-            for turn in range(2):
-                add_term(t, rec_sb[:, t, :], all_blocks)
+            add_term(t, rec_sb[:, t, :], all_blocks)
         for t in range(PACK):
             add_term(t, cubic[t][:], all_blocks)
         for t in (1, 2, 3):
             for side in range(2):
                 add_term(t, near[t][:, side, :], first_blocks, stop=(t, side) == (3, 1))
+        transpose_into(sums[3][:, blocks[1]], spare[:], False, False)
         for side in range(2):
             for t in (2, 1):
-                add_term(t, near[t][:, side, :], second_blocks)
+                add_term(t, near[t][:, side, :], (2,) if (t, side) == (2, 1) else second_blocks)
         for b in second_blocks:
             for side in range(2):
                 add_term(3, near[3][:, side, :], (b,), stop=side == 1)
@@ -194,8 +182,8 @@ def tile_picked_fhn8_none_p_kernel(tc, x_words, x_scales, w1, rec, gn, w2, offs,
         back = [bank(number) for number in BACK_BANKS]
         for b in all_blocks:
             z_turned = keep.tile([P, 2, P, 2], BF16, name="z_turned_%d" % b, align_bytes=64)
-            nc.vector.scalar_tensor_tensor(z_turned[:].rearrange("q u p e -> q (u p) e"), sums[b][:].rearrange("q (e c) -> q c e", e=2), 1.0,
-                                           window_0[:, S : 2 * S].rearrange("q (c e) -> q c e", e=2), ALU.subtract, ALU.mult)
+            nc.vector.tensor_tensor(z_turned[:].rearrange("q u p e -> q (u p) e"), sums[b][:].rearrange("q (e c) -> q c e", e=2),
+                                    window_0[:, S : 2 * S].rearrange("q (c e) -> q c e", e=2), ALU.mult)
             for u in range(2):
                 transpose_into(back[b][:, blocks[u]], z_turned[:, u].rearrange("q p e -> q (p e)").bitcast(F32), True, True)
 

@@ -41,6 +41,7 @@ def tile_picked_fhn8_none_p_kernel(tc, x_words, x_scales, w1, rec, gn, w2, offs,
 
     with ExitStack() as ctx:
         keep = ctx.enter_context(tc.tile_pool(name="keep", bufs=1))
+        shared = ctx.enter_context(tc.tile_pool(name="shared", bufs=1))
         psum = ctx.enter_context(tc.psum_pool(name="psum", bufs=1))
 
         def bank(number):
@@ -49,20 +50,27 @@ def tile_picked_fhn8_none_p_kernel(tc, x_words, x_scales, w1, rec, gn, w2, offs,
         offs_sb = keep.tile([P, S // GROUP], U16, name="offs_sb")
         west_sb = keep.tile([P, S // GROUP], U16, name="west_sb")
         east_sb = keep.tile([P, S // GROUP], U16, name="east_sb")
-        word_table = keep.tile([P, T], U32, name="word_table", tag="words_then_w1", align_bytes=64)
-        scale_table = keep.tile([P, T], U8, name="scale_table", align_bytes=64)
+        word_table = keep.tile([P, T], U32, name="word_table", align_bytes=64)
+        scale_table = shared.tile([P, T], U8, name="scale_table", offset=3072, align_bytes=64)
         w1_raw = keep.tile([P, PACK, H], F32, name="w1_raw", tag="w1_then_rec", align_bytes=64)
         gain = keep.tile([P, PACK], F32, name="gain")
 
-        nc.vector.memset(scale_table[:].bitcast(I32), 0)
+        nc.gpsimd.memset(scale_table[:].bitcast(I32), 0)
         nc.scalar.dma_start(gain[:], gn.rearrange("(p t) o -> p (t o)", t=PACK))
-        nc.sync.dma_start(w1_raw[:], w1.rearrange("(p j) c -> p j c", j=PACK))
+        w1_rows = w1.rearrange("(p j) c -> p j c", j=PACK)
+        nc.sync.dma_start(w1_raw[:, 0:2, :], w1_rows[:, 0:2, :])
         nc.sync.dma_start(offs_sb[:], offs)
-        for r in range(4):
-            nc.sync.dma_start(scale_table[r:P:QUADRANT, :].bitcast(I32), x_scales[0, r:16:4, :].bitcast(I32))
+        nc.sync.dma_start(scale_table[0:P:8, :].bitcast(I32), x_scales[0].bitcast(I32))
+        nc.sync.dma_start(w1_raw[:, 2:4, :], w1_rows[:, 2:4, :])
         nc.sync.dma_start(word_table[:].bitcast(I32), x_words[0].rearrange("p n t -> p (n t)").bitcast(I32))
+        picked_scale = keep.tile([P, S], U8, name="picked_scale", align_bytes=64)
+        nc.vector.tensor_copy(picked_scale[:], scale_table[:].indirect(offs_sb[:]))
+        x_scale = keep.tile([P, S], U8, name="x_scale", align_bytes=64)
+        nc.vector.memset(x_scale[:].bitcast(I32), 0)
+        for r in range(4):
+            nc.sync.dma_start(x_scale[r:P:QUADRANT, :].bitcast(I32), picked_scale[8 * r : P : QUADRANT, :].bitcast(I32))
         w2_rows = w2.rearrange("(p j) c -> p j c", j=PACK)
-        w2_raw = [keep.tile([P, PACK, HALF], F32, name="w2_raw_%d" % h, align_bytes=64) for h in range(2)]
+        w2_raw = [shared.tile([P, PACK, HALF], F32, name="w2_raw_%d" % h, offset=4096 * h, align_bytes=64) for h in range(2)]
         nc.sync.dma_start(w2_raw[0][:], w2_rows[:, :, halves[0]])
         nc.sync.dma_start(west_sb[:], west)
         nc.sync.dma_start(east_sb[:], east)
@@ -85,7 +93,8 @@ def tile_picked_fhn8_none_p_kernel(tc, x_words, x_scales, w1, rec, gn, w2, offs,
         w1_grouped, w1_codes, w1_scale = [], [], []
         for pair, interleave in enumerate((nc.vector.tensor_copy, nc.scalar.copy)):
             w1_grouped.append(keep.tile([P, 2, P, PACK], BF16, name="w1_grouped_%d" % pair, tag="w1_grouped_%d" % pair, align_bytes=64))
-            interleave(w1_grouped[pair][:].rearrange("p e m j -> p m j e"), w1_cols[:, :, :, 2 * pair : 2 * pair + 2])
+            for rows in ((slice(0, 4),), (slice(0, 2), slice(2, 4)))[pair]:
+                interleave(w1_grouped[pair][:].rearrange("p e m j -> p m j e")[:, :, rows, :], w1_cols[:, :, rows, 2 * pair : 2 * pair + 2])
 
         def quantise_w1(pair, tag):
             w1_codes.append(keep.tile([P, 2 * P], U32, name="w1_codes_%d" % pair, tag=tag, align_bytes=64))
@@ -94,12 +103,10 @@ def tile_picked_fhn8_none_p_kernel(tc, x_words, x_scales, w1, rec, gn, w2, offs,
                                   in_=w1_grouped[pair][:].rearrange("p e m j -> p (e m j)"))
 
         quantise_w1(0, "w1_codes_0")
-        x_scale = keep.tile([P, S], U8, name="x_scale", tag="w1_grouped_0", align_bytes=64)
-        nc.vector.tensor_copy(x_scale[:], scale_table[:].indirect(offs_sb[:]))
+        quantise_w1(1, "w1_codes_1")
         x_codes = keep.tile([P, S], U32, name="x_codes", align_bytes=64)
         for h in range(2):
             nc.vector.tensor_copy(x_codes[:, halves[h]], word_table[:].indirect(offs_sb[:, half_entries[h]]))
-        quantise_w1(1, "words_then_w1")
 
         rec_sb = keep.tile([P, PACK, S], F32, name="rec_sb", tag="w1_then_rec", align_bytes=64)
         rec_rows = rec.rearrange("(p t) s -> p t s", t=PACK)
@@ -119,10 +126,18 @@ def tile_picked_fhn8_none_p_kernel(tc, x_words, x_scales, w1, rec, gn, w2, offs,
                 nc.scalar.activation(signed_y[t][:, cols], acc[:, cols], ACT.Tanh)
             nc.scalar.activation(square[t][:], signed_y[t][:], ACT.Square, scale=math.sqrt(0.3125))
 
-        w2_grouped = keep.tile([P, N, PACK], BF16, name="w2_grouped", align_bytes=64)
+        w2_grouped, w2_codes, w2_scale = [], [], []
+
+        def quantise_w2(h, tag):
+            w2_codes.append(keep.tile([P, HALF], U32, name="w2_codes_%d" % h, tag=tag, align_bytes=64))
+            w2_scale.append(keep.tile([P, HALF], U8, name="w2_scale_%d" % h, align_bytes=64))
+            nc.vector.quantize_mx(out=w2_codes[h][:].bitcast(FP8X4), scales=w2_scale[h][:], in_=w2_grouped[h][:].rearrange("p c j -> p (c j)"))
+
         for h in range(2):
-            nc.vector.tensor_copy(w2_grouped[:, halves[h], :].rearrange("p (c i) j -> p c j i", i=4),
-                                  w2_raw[h][:].rearrange("p j (c i) -> p c j i", i=4))
+            w2_grouped.append(keep.tile([P, HALF, PACK], BF16, name="w2_grouped_%d" % h, align_bytes=64))
+            nc.vector.tensor_copy(w2_grouped[h][:].rearrange("p (c i) j -> p c j i", i=4), w2_raw[h][:].rearrange("p j (c i) -> p c j i", i=4))
+            if h == 0:
+                quantise_w2(0, "w2_codes_0")
 
         cubic, near = [], {}
 
@@ -145,9 +160,7 @@ def tile_picked_fhn8_none_p_kernel(tc, x_words, x_scales, w1, rec, gn, w2, offs,
         vector_neighbours(2, "square_3")
         spare = keep.tile([P, P], F32, name="spare", align_bytes=64)
         nc.scalar.activation(spare[:], signed_y[2][:].indirect(east_sb[:, blocks[3].start // GROUP : blocks[3].stop // GROUP]), ACT.Copy, scale=-0.25)
-        w2_codes = keep.tile([P, N], U32, name="w2_codes", tag="signed_y_2", align_bytes=64)
-        w2_scale = keep.tile([P, N], U8, name="w2_scale", align_bytes=64)
-        nc.vector.quantize_mx(out=w2_codes[:].bitcast(FP8X4), scales=w2_scale[:], in_=w2_grouped[:].rearrange("p c j -> p (c j)"))
+        quantise_w2(1, "signed_y_2")
         for t, cells in ((1, halves[0]), (3, halves[0]), (1, halves[1]), (3, blocks[2]), (3, blocks[3])):
             for side, places in enumerate((west_sb, east_sb)):
                 entries = slice(cells.start // GROUP, cells.stop // GROUP)
@@ -200,7 +213,7 @@ def tile_picked_fhn8_none_p_kernel(tc, x_words, x_scales, w1, rec, gn, w2, offs,
             for cells in parts:
                 for m in range(PACK):
                     place = slice(cells.start - halves[h].start, cells.stop - halves[h].start)
-                    nc.tensor.matmul_mx(out=accs[m][:, place], lhsT=w2_codes[:, blocks[m]].bitcast(FP8X4), lhsT_scale=w2_scale[:, blocks[m]],
+                    nc.tensor.matmul_mx(out=accs[m][:, place], lhsT=w2_codes[m // 2][:, blocks[m % 2]].bitcast(FP8X4), lhsT_scale=w2_scale[m // 2][:, blocks[m % 2]],
                                         rhs=z_codes[:, cells].bitcast(FP8X4), rhs_scale=z_scale[:, cells], start=True, stop=True)
             for m in range(PACK):
                 result = keep.tile([P, HALF], F32, name="result_%d_%d" % (h, m), align_bytes=64)

@@ -85,7 +85,7 @@ def tile_picked_fhn8_none_p_kernel(tc, x_words, x_scales, w1, rec, gn, w2, offs,
         gain_bank = bank(GAIN_BANK)
         for t in range(PACK):
             transpose_into(gain_bank[:, blocks[t]], gain[:, t : t + 1].to_broadcast([P, P]), True, True)
-        window_0 = keep.tile([P, 2 * S], F32, name="window_0", align_bytes=64)
+        window_0 = keep.tile([P, 2 * S], F32, name="window_0", tag="window_0", align_bytes=64)
         factor = window_0[:, S : 2 * S].rearrange("q (u p e) -> q u p e", u=2, e=2)
         nc.scalar.activation(factor, gain_bank[:].rearrange("q (u e p) -> q u p e", u=2, e=2), ACT.Copy, scale=-1.0)
 
@@ -117,14 +117,26 @@ def tile_picked_fhn8_none_p_kernel(tc, x_words, x_scales, w1, rec, gn, w2, offs,
         for t in range(PACK):
             signed_y.append(keep.tile([P, S], F32, name="signed_y_%d" % t, tag="signed_y_%d" % t, align_bytes=64) if t > 0 else window_0[:, 0:S])
             square.append(keep.tile([P, S], F32, name="square_%d" % t, tag="square_%d" % t, align_bytes=64))
-            width = S // len(FIRST_BANKS[t])
-            for part, number in enumerate(FIRST_BANKS[t]):
-                cols = slice(part * width, (part + 1) * width)
-                acc = bank(number)
-                nc.tensor.matmul_mx(out=acc[:, cols], lhsT=w1_codes[t // 2][:, blocks[t % 2]].bitcast(FP8X4), lhsT_scale=w1_scale[t // 2][:, blocks[t % 2]],
-                                    rhs=x_codes[:, cols].bitcast(FP8X4), rhs_scale=x_scale[:, cols], start=True, stop=True)
-                nc.scalar.activation(signed_y[t][:, cols], acc[:, cols], ACT.Tanh)
+
+        def first_product(t, cols, number):
+            acc = bank(number)
+            nc.tensor.matmul_mx(out=acc[:, cols], lhsT=w1_codes[t // 2][:, blocks[t % 2]].bitcast(FP8X4), lhsT_scale=w1_scale[t // 2][:, blocks[t % 2]],
+                                rhs=x_codes[:, cols].bitcast(FP8X4), rhs_scale=x_scale[:, cols], start=True, stop=True)
+            nc.scalar.activation(signed_y[t][:, cols], acc[:, cols], ACT.Tanh)
+
+        def make_square(t):
             nc.scalar.activation(square[t][:], signed_y[t][:], ACT.Square, scale=math.sqrt(0.3125))
+
+        first_product(0, halves[0], 1)
+        first_product(1, halves[0], 6)
+        first_product(0, halves[1], 7)
+        first_product(1, halves[1], 2)
+        make_square(0)
+        first_product(2, slice(0, S), 3)
+        make_square(1)
+        first_product(3, slice(0, S), 4)
+        make_square(2)
+        make_square(3)
 
         w2_grouped, w2_codes, w2_scale = [], [], []
 
@@ -133,11 +145,13 @@ def tile_picked_fhn8_none_p_kernel(tc, x_words, x_scales, w1, rec, gn, w2, offs,
             w2_scale.append(keep.tile([P, HALF], U8, name="w2_scale_%d" % h, align_bytes=64))
             nc.vector.quantize_mx(out=w2_codes[h][:].bitcast(FP8X4), scales=w2_scale[h][:], in_=w2_grouped[h][:].rearrange("p c j -> p (c j)"))
 
-        for h in range(2):
-            w2_grouped.append(keep.tile([P, HALF, PACK], BF16, name="w2_grouped_%d" % h, align_bytes=64))
-            nc.vector.tensor_copy(w2_grouped[h][:].rearrange("p (c i) j -> p c j i", i=4), w2_raw[h][:].rearrange("p j (c i) -> p c j i", i=4))
-            if h == 0:
-                quantise_w2(0, "w2_codes_0")
+        w2_grouped.append(keep.tile([P, HALF, PACK], BF16, name="w2_grouped_0", align_bytes=64))
+
+        def cast_w2(h, cols, move):
+            move(w2_grouped[h][:, cols, :].rearrange("p (c i) j -> p c j i", i=4), w2_raw[h][:, :, cols].rearrange("p j (c i) -> p c j i", i=4))
+
+        cast_w2(0, halves[0], nc.vector.tensor_copy)
+        quantise_w2(0, "w2_codes_0")
 
         cubic, near = [], {}
 
@@ -145,7 +159,7 @@ def tile_picked_fhn8_none_p_kernel(tc, x_words, x_scales, w1, rec, gn, w2, offs,
             near[t] = keep.tile([P, 2, S], F32, name="near_%d" % t, tag=tag, align_bytes=64)
             for h in range(2):
                 for side, places in enumerate((west_sb, east_sb)):
-                    cells = blocks[2] if (h, side) == (1, 1) else halves[h]
+                    cells = halves[h]
                     window = signed_y[t][:].indirect(places[:, cells.start // GROUP : cells.stop // GROUP])
                     nc.vector.tensor_scalar(near[t][:, side, cells], window, -0.25, 0.0, ALU.mult, ALU.add)
 
@@ -157,14 +171,15 @@ def tile_picked_fhn8_none_p_kernel(tc, x_words, x_scales, w1, rec, gn, w2, offs,
                 near[t] = keep.tile([P, 2, S], F32, name="near_%d" % t, align_bytes=64)
             cubic.append(keep.tile([P, S], F32, name="cubic_%d" % t, align_bytes=64))
             nc.vector.scalar_tensor_tensor(cubic[t][:], square[t][:], 1.0, signed_y[t][:], ALU.subtract, ALU.mult)
+        w2_grouped.append(keep.tile([P, HALF, PACK], BF16, name="w2_grouped_1", tag="square_2", align_bytes=64))
+        cast_w2(1, blocks[0], nc.vector.tensor_copy)
         vector_neighbours(2, "square_3")
-        spare = keep.tile([P, P], F32, name="spare", align_bytes=64)
-        nc.scalar.activation(spare[:], signed_y[2][:].indirect(east_sb[:, blocks[3].start // GROUP : blocks[3].stop // GROUP]), ACT.Copy, scale=-0.25)
-        quantise_w2(1, "signed_y_2")
         for t, cells in ((1, halves[0]), (3, halves[0]), (1, halves[1]), (3, blocks[2]), (3, blocks[3])):
             for side, places in enumerate((west_sb, east_sb)):
                 entries = slice(cells.start // GROUP, cells.stop // GROUP)
                 nc.scalar.activation(near[t][:, side, cells], signed_y[t][:].indirect(places[:, entries]), ACT.Copy, scale=-0.25)
+
+        cast_w2(1, blocks[1], nc.scalar.copy)
 
         sums = [bank(number) for number in SUM_BANKS]
 
@@ -184,10 +199,9 @@ def tile_picked_fhn8_none_p_kernel(tc, x_words, x_scales, w1, rec, gn, w2, offs,
         for t in (1, 2, 3):
             for side in range(2):
                 add_term(t, near[t][:, side, :], first_blocks, stop=(t, side) == (3, 1))
-        transpose_into(sums[3][:, blocks[1]], spare[:], False, False)
         for side in range(2):
             for t in (2, 1):
-                add_term(t, near[t][:, side, :], (2,) if (t, side) == (2, 1) else second_blocks)
+                add_term(t, near[t][:, side, :], second_blocks)
         for b in second_blocks:
             for side in range(2):
                 add_term(3, near[3][:, side, :], (b,), stop=side == 1)
@@ -207,6 +221,8 @@ def tile_picked_fhn8_none_p_kernel(tc, x_words, x_scales, w1, rec, gn, w2, offs,
             nc.scalar.copy(z_grouped[:].bitcast(F32).rearrange("p (c u) -> p c u", u=2),
                            back[b][:, 0 : 2 * P].rearrange("p (u c) -> p c u", u=2))
             nc.vector.quantize_mx(out=z_codes[:, blocks[b]].bitcast(FP8X4), scales=z_scale[:, blocks[b]], in_=z_grouped[:])
+            if b == 1:
+                quantise_w2(1, "window_0")
 
         for h, parts in enumerate(((halves[0],), (blocks[2], blocks[3]))):
             accs = [bank(number) for number in OUT_BANKS[h]]

@@ -218,22 +218,38 @@ def tile_picked_fhn8_none_p_kernel(tc, x_words, x_scales, w1, rec, gn, w2, offs,
         z_scale = keep.tile([P, S], U8, name="z_scale", align_bytes=64)
         for b in all_blocks:
             z_grouped = keep.tile([P, P * PACK], BF16, name="z_grouped_%d" % b, align_bytes=64)
-            nc.scalar.copy(z_grouped[:].bitcast(F32).rearrange("p (c u) -> p c u", u=2),
+            unpack = nc.vector.tensor_copy if b == 3 else nc.scalar.copy
+            unpack(z_grouped[:].bitcast(F32).rearrange("p (c u) -> p c u", u=2),
                            back[b][:, 0 : 2 * P].rearrange("p (u c) -> p c u", u=2))
             nc.vector.quantize_mx(out=z_codes[:, blocks[b]].bitcast(FP8X4), scales=z_scale[:, blocks[b]], in_=z_grouped[:])
             if b == 1:
                 quantise_w2(1, "window_0")
 
-        for h, parts in enumerate(((halves[0],), (blocks[2], blocks[3]))):
-            accs = [bank(number) for number in OUT_BANKS[h]]
-            for cells in parts:
-                for m in range(PACK):
-                    place = slice(cells.start - halves[h].start, cells.stop - halves[h].start)
-                    nc.tensor.matmul_mx(out=accs[m][:, place], lhsT=w2_codes[m // 2][:, blocks[m % 2]].bitcast(FP8X4), lhsT_scale=w2_scale[m // 2][:, blocks[m % 2]],
-                                        rhs=z_codes[:, cells].bitcast(FP8X4), rhs_scale=z_scale[:, cells], start=True, stop=True)
-            for m in range(PACK):
-                result = keep.tile([P, HALF], F32, name="result_%d_%d" % (h, m), align_bytes=64)
-                empty = nc.vector.tensor_copy if (h == 1 and m % 2 == 1) else nc.scalar.copy
-                empty(result[:], accs[m][:, 0:HALF])
-                queue = nc.scalar if (h, m) == (1, 2) else nc.sync
-                queue.dma_start(out[blocks[m], halves[h]], result[:])
+        out_rows = out.rearrange("(m p) c -> p m c", p=P)
+
+        def multiply(cells, tiles, number):
+            acc = bank(number)
+            width = cells.stop - cells.start
+            for i, m in enumerate(tiles):
+                nc.tensor.matmul_mx(out=acc[:, i * width : (i + 1) * width], lhsT=w2_codes[m // 2][:, blocks[m % 2]].bitcast(FP8X4),
+                                    lhsT_scale=w2_scale[m // 2][:, blocks[m % 2]],
+                                    rhs=z_codes[:, cells].bitcast(FP8X4), rhs_scale=z_scale[:, cells], start=True, stop=True)
+            return acc[:, 0 : len(tiles) * width].rearrange("p (m c) -> p m c", c=width)
+
+        def send(cells, tiles, number, empty, queue):
+            result = keep.tile([P, len(tiles), cells.stop - cells.start], F32, name="result_%d_%d" % (cells.start, tiles[0]), align_bytes=64)
+            empty(result[:], multiply(cells, tiles, number))
+            queue.dma_start(out_rows[:, tiles[0] : tiles[-1] + 1, cells], result[:])
+
+        send(blocks[0], (0,), 5, nc.scalar.copy, nc.sync)
+        send(blocks[0], (1,), 6, nc.scalar.copy, nc.sync)
+        send(blocks[1], (0, 1), 7, nc.scalar.copy, nc.sync)
+        send(halves[0], (2,), 0, nc.scalar.copy, nc.sync)
+        send(halves[0], (3,), 1, nc.scalar.copy, nc.sync)
+        second = keep.tile([P, PACK, HALF], F32, name="second", align_bytes=64)
+        for pair, number in enumerate((5, 2)):
+            nc.vector.tensor_copy(second[:, 2 * pair : 2 * pair + 2, blocks[0]], multiply(blocks[2], (2 * pair, 2 * pair + 1), number))
+        for m, number in enumerate((3, 4, 6, 7)):
+            empty, queue = ((nc.scalar.copy, nc.scalar), (nc.vector.tensor_copy, nc.sync))[m % 2]
+            empty(second[:, m : m + 1, blocks[1]], multiply(blocks[3], (m,), number))
+            queue.dma_start(out_rows[:, m : m + 1, halves[1]], second[:, m : m + 1, :])

@@ -110,8 +110,8 @@ def tile_picked_fhn8_none_p_kernel(tc, x_words, x_scales, w1, rec, gn, w2, offs,
 
         rec_sb = keep.tile([P, PACK, S], F32, name="rec_sb", tag="w1_then_rec", align_bytes=64)
         rec_rows = rec.rearrange("(p t) s -> p t s", t=PACK)
-        for t in VECTOR_PLANES + SCALAR_PLANES:
-            nc.sync.dma_start(rec_sb[:, t, :], rec_rows[:, t, :])
+        for e in range(2):
+            nc.sync.dma_start(rec_sb[:, e:PACK:2, :], rec_rows[:, e:PACK:2, :])
 
         signed_y, square = [], []
         for t in range(PACK):
@@ -181,14 +181,39 @@ def tile_picked_fhn8_none_p_kernel(tc, x_words, x_scales, w1, rec, gn, w2, offs,
 
         cast_w2(1, blocks[1], nc.scalar.copy)
 
-        sums = [bank(number) for number in SUM_BANKS]
+        sums = [bank(number) for number in (5, 6, 7, 0, 1)]
 
         def add_term(t, term, where, start=False, stop=False):
             for b in where:
-                transpose_into(sums[b][:, blocks[2 * (t % 2) + t // 2]], term[:, blocks[b]], start, stop)
+                if b < 3:
+                    transpose_into(sums[b][:, blocks[2 * (t % 2) + t // 2]], term[:, blocks[b]], start and t == 0, stop)
+                else:
+                    transpose_into(sums[3 + t // 2][:, blocks[t % 2]], term[:, blocks[b]], start, stop)
+
+        back = {}
+        z_codes = keep.tile([P, S], U32, name="z_codes", align_bytes=64)
+        z_scale = keep.tile([P, S], U8, name="z_scale", align_bytes=64)
+
+        def leave(b, number):
+            back[b] = bank(number)
+            z_turned = keep.tile([P, 2, P, 2], BF16, name="z_turned_%d" % b, tag="z_turned_%d" % b, align_bytes=64)
+            nc.vector.tensor_tensor(z_turned[:].rearrange("q u p e -> q (u p) e"), sums[b][:].rearrange("q (e c) -> q c e", e=2),
+                                    window_0[:, S : 2 * S].rearrange("q (c e) -> q c e", e=2), ALU.mult)
+            for u in range(2):
+                transpose_into(back[b][:, blocks[u]], z_turned[:, u].rearrange("q p e -> q (p e)").bitcast(F32), True, True)
+
+        def leave_last(u, tag):
+            z_turned = keep.tile([P, P, 2], BF16, name="z_last_%d" % u, tag=tag, align_bytes=64)
+            nc.vector.tensor_tensor(z_turned[:], sums[3 + u][:, halves[0]].rearrange("q (e p) -> q p e", e=2), factor[:, u], ALU.mult)
+            transpose_into(back[3][:, blocks[u]], z_turned[:].rearrange("q p e -> q (p e)").bitcast(F32), True, True)
+
+        def quantise_z(b, unpack):
+            z_grouped = keep.tile([P, P * PACK], BF16, name="z_grouped_%d" % b, tag="z_grouped_%d" % b, align_bytes=64)
+            unpack(z_grouped[:].bitcast(F32).rearrange("p (c u) -> p c u", u=2), back[b][:, 0 : 2 * P].rearrange("p (u c) -> p c u", u=2))
+            nc.vector.quantize_mx(out=z_codes[:, blocks[b]].bitcast(FP8X4), scales=z_scale[:, blocks[b]], in_=z_grouped[:])
 
         for t in VECTOR_PLANES:
-            add_term(t, rec_sb[:, t, :], all_blocks, start=t == 0)
+            add_term(t, rec_sb[:, t, :], all_blocks, start=True)
         for where in (first_blocks, second_blocks):
             for side in range(2):
                 add_term(0, near[0][:, side, :], where)
@@ -200,30 +225,24 @@ def tile_picked_fhn8_none_p_kernel(tc, x_words, x_scales, w1, rec, gn, w2, offs,
             for side in range(2):
                 add_term(t, near[t][:, side, :], first_blocks, stop=(t, side) == (3, 1))
         for side in range(2):
-            for t in (2, 1):
-                add_term(t, near[t][:, side, :], second_blocks)
-        for b in second_blocks:
-            for side in range(2):
-                add_term(3, near[3][:, side, :], (b,), stop=side == 1)
-
-        back = [bank(number) for number in BACK_BANKS]
-        for b in all_blocks:
-            z_turned = keep.tile([P, 2, P, 2], BF16, name="z_turned_%d" % b, align_bytes=64)
-            nc.vector.tensor_tensor(z_turned[:].rearrange("q u p e -> q (u p) e"), sums[b][:].rearrange("q (e c) -> q c e", e=2),
-                                    window_0[:, S : 2 * S].rearrange("q (c e) -> q c e", e=2), ALU.mult)
-            for u in range(2):
-                transpose_into(back[b][:, blocks[u]], z_turned[:, u].rearrange("q p e -> q (p e)").bitcast(F32), True, True)
-
-        z_codes = keep.tile([P, S], U32, name="z_codes", align_bytes=64)
-        z_scale = keep.tile([P, S], U8, name="z_scale", align_bytes=64)
-        for b in all_blocks:
-            z_grouped = keep.tile([P, P * PACK], BF16, name="z_grouped_%d" % b, align_bytes=64)
-            unpack = nc.vector.tensor_copy if b == 3 else nc.scalar.copy
-            unpack(z_grouped[:].bitcast(F32).rearrange("p (c u) -> p c u", u=2),
-                           back[b][:, 0 : 2 * P].rearrange("p (u c) -> p c u", u=2))
-            nc.vector.quantize_mx(out=z_codes[:, blocks[b]].bitcast(FP8X4), scales=z_scale[:, blocks[b]], in_=z_grouped[:])
-            if b == 1:
-                quantise_w2(1, "window_0")
+            add_term(2, near[2][:, side, :], second_blocks)
+            add_term(1, near[1][:, side, :], (2,))
+            add_term(1, near[1][:, side, :], (3,), stop=side == 1)
+        for side in range(2):
+            add_term(3, near[3][:, side, :], (2,), stop=side == 1)
+        leave(0, 2)
+        for side in range(2):
+            add_term(3, near[3][:, side, :], (3,), stop=side == 1)
+        leave(1, 3)
+        leave(2, 4)
+        back[3] = bank(5)
+        leave_last(0, "z_last_0")
+        quantise_z(0, nc.scalar.copy)
+        leave_last(1, "z_turned_1")
+        quantise_z(1, nc.scalar.copy)
+        quantise_w2(1, "window_0")
+        quantise_z(2, nc.scalar.copy)
+        quantise_z(3, nc.vector.tensor_copy)
 
         out_rows = out.rearrange("(m p) c -> p m c", p=P)
 
@@ -241,15 +260,14 @@ def tile_picked_fhn8_none_p_kernel(tc, x_words, x_scales, w1, rec, gn, w2, offs,
             empty(result[:], multiply(cells, tiles, number))
             queue.dma_start(out_rows[:, tiles[0] : tiles[-1] + 1, cells], result[:])
 
-        send(blocks[0], (0,), 5, nc.scalar.copy, nc.sync)
-        send(blocks[0], (1,), 6, nc.scalar.copy, nc.sync)
+        send(blocks[0], (0, 1), 6, nc.scalar.copy, nc.sync)
         send(blocks[1], (0, 1), 7, nc.scalar.copy, nc.sync)
         send(halves[0], (2,), 0, nc.scalar.copy, nc.sync)
-        send(halves[0], (3,), 1, nc.scalar.copy, nc.sync)
+        send(halves[0], (3,), 2, nc.scalar.copy, nc.sync)
         second = keep.tile([P, PACK, HALF], F32, name="second", align_bytes=64)
-        for pair, number in enumerate((5, 2)):
+        for pair, number in enumerate((1, 3)):
             nc.vector.tensor_copy(second[:, 2 * pair : 2 * pair + 2, blocks[0]], multiply(blocks[2], (2 * pair, 2 * pair + 1), number))
-        for m, number in enumerate((3, 4, 6, 7)):
+        for m, number in enumerate((4, 5, 6, 7)):
             empty, queue = ((nc.scalar.copy, nc.scalar), (nc.vector.tensor_copy, nc.sync))[m % 2]
             empty(second[:, m : m + 1, blocks[1]], multiply(blocks[3], (m,), number))
             queue.dma_start(out_rows[:, m : m + 1, halves[1]], second[:, m : m + 1, :])

@@ -264,10 +264,8 @@ def tile_picked_fhn8_none_p_kernel(tc, x_words, x_scales, w1, rec, gn, w2, offs,
         send(blocks[1], (0, 1), 7, nc.scalar.copy, nc.sync)
         send(halves[0], (2,), 0, nc.scalar.copy, nc.sync)
         send(halves[0], (3,), 2, nc.scalar.copy, nc.sync)
-        second = keep.tile([P, PACK, HALF], F32, name="second", align_bytes=64)
         for pair, number in enumerate((1, 3)):
-            nc.vector.tensor_copy(second[:, 2 * pair : 2 * pair + 2, blocks[0]], multiply(blocks[2], (2 * pair, 2 * pair + 1), number))
+            send(blocks[2], (2 * pair, 2 * pair + 1), number, nc.vector.tensor_copy, nc.sync)
         for m, number in enumerate((4, 5, 6, 7)):
             empty, queue = ((nc.scalar.copy, nc.scalar), (nc.vector.tensor_copy, nc.sync))[m % 2]
-            empty(second[:, m : m + 1, blocks[1]], multiply(blocks[3], (m,), number))
-            queue.dma_start(out_rows[:, m : m + 1, halves[1]], second[:, m : m + 1, :])
+            send(blocks[3], (m,), number, empty, queue)

@@ -266,6 +266,5 @@ def tile_picked_fhn8_none_p_kernel(tc, x_words, x_scales, w1, rec, gn, w2, offs,
         send(halves[0], (3,), 2, nc.scalar.copy, nc.sync)
         for pair, number in enumerate((1, 3)):
             send(blocks[2], (2 * pair, 2 * pair + 1), number, nc.vector.tensor_copy, nc.sync)
-        for m, number in enumerate((4, 5, 6, 7)):
-            empty, queue = ((nc.scalar.copy, nc.scalar), (nc.vector.tensor_copy, nc.sync))[m % 2]
-            send(blocks[3], (m,), number, empty, queue)
+        send(blocks[3], (0, 1), 4, nc.scalar.copy, nc.scalar)
+        send(blocks[3], (2, 3), 5, nc.vector.tensor_copy, nc.sync)

@@ -221,13 +221,15 @@ def tile_picked_fhn8_none_p_kernel(tc, x_words, x_scales, w1, rec, gn, w2, offs,
             add_term(t, rec_sb[:, t, :], all_blocks)
         for t in range(PACK):
             add_term(t, cubic[t][:], all_blocks)
-        for t in (1, 2, 3):
-            for side in range(2):
-                add_term(t, near[t][:, side, :], first_blocks, stop=(t, side) == (3, 1))
         for side in range(2):
-            add_term(2, near[2][:, side, :], second_blocks)
+            add_term(1, near[1][:, side, :], first_blocks)
+        for side in range(2):
+            for t in (3, 2):
+                add_term(t, near[t][:, side, :], first_blocks, stop=(t, side) == (2, 1))
+        for side in range(2):
             add_term(1, near[1][:, side, :], (2,))
             add_term(1, near[1][:, side, :], (3,), stop=side == 1)
+            add_term(2, near[2][:, side, :], second_blocks)
         for side in range(2):
             add_term(3, near[3][:, side, :], (2,), stop=side == 1)
         leave(0, 2)

@@ -20,6 +20,7 @@ PACK = 4
 GROUP = 16
 QUADRANT = 32
 HALF = S // 2
+SPLIT = 208
 VECTOR_PLANES = (0, 2)
 SCALAR_PLANES = (1, 3)
 
@@ -114,9 +115,10 @@ def tile_picked_fhn8_none_p_kernel(tc, x_words, x_scales, w1, rec, gn, w2, offs,
             nc.sync.dma_start(rec_sb[:, e:PACK:2, :], rec_rows[:, e:PACK:2, :])
 
         signed_y, square = [], []
+        window_2 = keep.tile([P, 2 * S], F32, name="window_2", tag="window_2", align_bytes=64)
         for t in range(PACK):
-            signed_y.append(keep.tile([P, S], F32, name="signed_y_%d" % t, tag="signed_y_%d" % t, align_bytes=64) if t > 0 else window_0[:, 0:S])
-            square.append(keep.tile([P, S], F32, name="square_%d" % t, tag="square_%d" % t, align_bytes=64))
+            signed_y.append(keep.tile([P, S], F32, name="signed_y_%d" % t, align_bytes=64) if t % 2 else (window_0, window_2)[t // 2][:, 0:S])
+            square.append(keep.tile([P, S], F32, name="square_%d" % t, align_bytes=64) if t < 3 else window_2[:, S : 2 * S])
 
         def first_product(t, cols, number):
             acc = bank(number)
@@ -160,7 +162,7 @@ def tile_picked_fhn8_none_p_kernel(tc, x_words, x_scales, w1, rec, gn, w2, offs,
             for h in range(2):
                 for side, places in enumerate((west_sb, east_sb)):
                     cells = halves[h]
-                    window = signed_y[t][:].indirect(places[:, cells.start // GROUP : cells.stop // GROUP])
+                    window = window_2[:].indirect(places[:, cells.start // GROUP : cells.stop // GROUP])
                     nc.vector.tensor_scalar(near[t][:, side, cells], window, -0.25, 0.0, ALU.mult, ALU.add)
 
         near[0] = keep.tile([P, 2, S], F32, name="near_0", align_bytes=64)
@@ -171,15 +173,16 @@ def tile_picked_fhn8_none_p_kernel(tc, x_words, x_scales, w1, rec, gn, w2, offs,
                 near[t] = keep.tile([P, 2, S], F32, name="near_%d" % t, align_bytes=64)
             cubic.append(keep.tile([P, S], F32, name="cubic_%d" % t, align_bytes=64))
             nc.vector.scalar_tensor_tensor(cubic[t][:], square[t][:], 1.0, signed_y[t][:], ALU.subtract, ALU.mult)
-        w2_grouped.append(keep.tile([P, HALF, PACK], BF16, name="w2_grouped_1", tag="square_2", align_bytes=64))
-        cast_w2(1, blocks[0], nc.vector.tensor_copy)
-        vector_neighbours(2, "square_3")
+        vector_neighbours(2, "near_2")
+        w2_grouped.append(keep.tile([P, HALF, PACK], BF16, name="w2_grouped_1", tag="window_2", align_bytes=64))
+        nc.gpsimd.tensor_scalar(w2_grouped[1][:, 0:SPLIT, :], w2_raw[1][:, :, 0:SPLIT].rearrange("p j c -> p c j"), 1.0, 0.0, ALU.mult, ALU.add)
         for t, cells in ((1, halves[0]), (3, halves[0]), (1, halves[1]), (3, blocks[2]), (3, blocks[3])):
             for side, places in enumerate((west_sb, east_sb)):
                 entries = slice(cells.start // GROUP, cells.stop // GROUP)
                 nc.scalar.activation(near[t][:, side, cells], signed_y[t][:].indirect(places[:, entries]), ACT.Copy, scale=-0.25)
 
-        cast_w2(1, blocks[1], nc.scalar.copy)
+
+        cast_w2(1, slice(SPLIT, HALF), nc.scalar.copy)
 
         sums = [bank(number) for number in (5, 6, 7, 0, 1)]
 
@@ -214,15 +217,15 @@ def tile_picked_fhn8_none_p_kernel(tc, x_words, x_scales, w1, rec, gn, w2, offs,
 
         for t in VECTOR_PLANES:
             add_term(t, rec_sb[:, t, :], all_blocks, start=True)
-        for where in (first_blocks, second_blocks):
-            for side in range(2):
-                add_term(0, near[0][:, side, :], where)
+        add_term(0, near[0][:, 0, :], all_blocks)
         for t in SCALAR_PLANES:
             add_term(t, rec_sb[:, t, :], all_blocks)
-        for t in range(PACK):
+        add_term(0, near[0][:, 1, :], all_blocks)
+        for t in range(2):
             add_term(t, cubic[t][:], all_blocks)
         for side in range(2):
             add_term(1, near[1][:, side, :], first_blocks)
+            add_term(2 + side, cubic[2 + side][:], all_blocks)
         for side in range(2):
             for t in (3, 2):
                 add_term(t, near[t][:, side, :], first_blocks, stop=(t, side) == (2, 1))

@@ -150,7 +150,7 @@ def tile_picked_fhn8_none_p_kernel(tc, x_words, x_scales, w1, rec, gn, w2, offs,
         w2_grouped.append(keep.tile([P, HALF, PACK], BF16, name="w2_grouped_0", align_bytes=64))
 
         def cast_w2(h, cols, move):
-            move(w2_grouped[h][:, cols, :].rearrange("p (c i) j -> p c j i", i=4), w2_raw[h][:, :, cols].rearrange("p j (c i) -> p c j i", i=4))
+            move(w2_grouped[h][:, cols, :], w2_raw[h][:, :, cols].rearrange("p j c -> p c j"))
 
         cast_w2(0, halves[0], nc.vector.tensor_copy)
         quantise_w2(0, "w2_codes_0")

@@ -269,7 +269,9 @@ def tile_picked_fhn8_none_p_kernel(tc, x_words, x_scales, w1, rec, gn, w2, offs,
         send(blocks[1], (0, 1), 7, nc.scalar.copy, nc.sync)
         send(halves[0], (2,), 0, nc.scalar.copy, nc.sync)
         send(halves[0], (3,), 2, nc.scalar.copy, nc.sync)
+        late = [keep.tile([P, 2, HALF], F32, name="late_%d" % pair, align_bytes=64) for pair in range(2)]
         for pair, number in enumerate((1, 3)):
-            send(blocks[2], (2 * pair, 2 * pair + 1), number, nc.vector.tensor_copy, nc.sync)
-        send(blocks[3], (0, 1), 4, nc.scalar.copy, nc.scalar)
-        send(blocks[3], (2, 3), 5, nc.vector.tensor_copy, nc.sync)
+            nc.vector.tensor_copy(late[pair][:, :, blocks[0]], multiply(blocks[2], (2 * pair, 2 * pair + 1), number))
+        for pair, (number, empty, queue) in enumerate(((4, nc.scalar.copy, nc.scalar), (5, nc.vector.tensor_copy, nc.sync))):
+            empty(late[pair][:, :, blocks[1]], multiply(blocks[3], (2 * pair, 2 * pair + 1), number))
+            queue.dma_start(out_rows[:, 2 * pair : 2 * pair + 2, halves[1]], late[pair][:])

@@ -272,6 +272,8 @@ def tile_picked_fhn8_none_p_kernel(tc, x_words, x_scales, w1, rec, gn, w2, offs,
         late = [keep.tile([P, 2, HALF], F32, name="late_%d" % pair, align_bytes=64) for pair in range(2)]
         for pair, number in enumerate((1, 3)):
             nc.vector.tensor_copy(late[pair][:, :, blocks[0]], multiply(blocks[2], (2 * pair, 2 * pair + 1), number))
-        for pair, (number, empty, queue) in enumerate(((4, nc.scalar.copy, nc.scalar), (5, nc.vector.tensor_copy, nc.sync))):
-            empty(late[pair][:, :, blocks[1]], multiply(blocks[3], (2 * pair, 2 * pair + 1), number))
-            queue.dma_start(out_rows[:, 2 * pair : 2 * pair + 2, halves[1]], late[pair][:])
+        for m, (number, empty, queue) in enumerate(((4, nc.scalar.copy, nc.sync), (5, nc.vector.tensor_copy, nc.sync),
+                                                    (6, nc.scalar.copy, nc.scalar), (7, nc.vector.tensor_copy, nc.sync))):
+            row = late[m // 2][:, m % 2 : m % 2 + 1, :]
+            empty(row[:, :, blocks[1]], multiply(blocks[3], (m,), number))
+            queue.dma_start(out_rows[:, m : m + 1, halves[1]], row)

@@ -142,28 +142,28 @@ def tile_picked_fhn8_none_p_kernel(tc, x_words, x_scales, w1, rec, gn, w2, offs,
 
         w2_grouped, w2_codes, w2_scale = [], [], []
 
-        def quantise_w2(h, tag):
+        def quantise_w2(h, tag, pieces):
             w2_codes.append(keep.tile([P, HALF], U32, name="w2_codes_%d" % h, tag=tag, align_bytes=64))
             w2_scale.append(keep.tile([P, HALF], U8, name="w2_scale_%d" % h, align_bytes=64))
-            nc.vector.quantize_mx(out=w2_codes[h][:].bitcast(FP8X4), scales=w2_scale[h][:], in_=w2_grouped[h][:].rearrange("p c j -> p (c j)"))
+            for cols in pieces:
+                nc.vector.quantize_mx(out=w2_codes[h][:, cols].bitcast(FP8X4), scales=w2_scale[h][:, cols], in_=w2_grouped[h][:, cols, :].rearrange("p c j -> p (c j)"))
 
         w2_grouped.append(keep.tile([P, HALF, PACK], BF16, name="w2_grouped_0", align_bytes=64))
 
         def cast_w2(h, cols, move):
             move(w2_grouped[h][:, cols, :], w2_raw[h][:, :, cols].rearrange("p j c -> p c j"))
 
-        cast_w2(0, halves[0], nc.vector.tensor_copy)
-        quantise_w2(0, "w2_codes_0")
+        for m in range(2):
+            cast_w2(0, blocks[m], nc.vector.tensor_copy)
+        quantise_w2(0, "w2_codes_0", blocks[0:2])
 
         cubic, near = [], {}
 
         def vector_neighbours(t, tag):
             near[t] = keep.tile([P, 2, S], F32, name="near_%d" % t, tag=tag, align_bytes=64)
-            for h in range(2):
-                for side, places in enumerate((west_sb, east_sb)):
-                    cells = halves[h]
-                    window = window_2[:].indirect(places[:, cells.start // GROUP : cells.stop // GROUP])
-                    nc.vector.tensor_scalar(near[t][:, side, cells], window, -0.25, 0.0, ALU.mult, ALU.add)
+            for side, cells in ((0, slice(0, S)), (1, halves[0]), (1, halves[1])):
+                window = window_2[:].indirect((west_sb, east_sb)[side][:, cells.start // GROUP : cells.stop // GROUP])
+                nc.vector.tensor_scalar(near[t][:, side, cells], window, -0.25, 0.0, ALU.mult, ALU.add)
 
         near[0] = keep.tile([P, 2, S], F32, name="near_0", align_bytes=64)
         for side, places in enumerate((west_sb, east_sb)):
@@ -245,7 +245,7 @@ def tile_picked_fhn8_none_p_kernel(tc, x_words, x_scales, w1, rec, gn, w2, offs,
         quantise_z(0, nc.scalar.copy)
         leave_last(1, "z_turned_1")
         quantise_z(1, nc.scalar.copy)
-        quantise_w2(1, "window_0")
+        quantise_w2(1, "window_0", halves[0:1])
         quantise_z(2, nc.scalar.copy)
         quantise_z(3, nc.vector.tensor_copy)
 

import math
from contextlib import ExitStack

import concourse.mybir as mybir
from concourse.masks import make_identity

F32 = mybir.dt.float32
BF16 = mybir.dt.bfloat16
I32 = mybir.dt.int32
U32 = mybir.dt.uint32
U16 = mybir.dt.uint16
U8 = mybir.dt.uint8
FP8X4 = mybir.dt.float8_e4m3fn_x4
ALU = mybir.AluOpType
ACT = mybir.ActivationFunctionType

K, T, S, N, H = 512, 2048, 512, 512, 512
P = 128
PACK = 4
GROUP = 16
QUADRANT = 32
HALF = S // 2
SPLIT = 208
VECTOR_PLANES = (0, 2)
SCALAR_PLANES = (1, 3)

GAIN_BANK = 0
FIRST_BANKS = ((1, 7), (2,), (3,), (4,))
SUM_BANKS = (5, 6, 7, 0)
BACK_BANKS = (1, 2, 3, 4)
OUT_BANKS = (SUM_BANKS, BACK_BANKS)

FLOPS = 2 * K * H * S + 2 * H * N * S


def tile_picked_fhn8_none_p_kernel(tc, x_words, x_scales, w1, rec, gn, w2, offs, west, east, out):
    nc = tc.nc
    halves = [slice(h * HALF, (h + 1) * HALF) for h in range(2)]
    half_entries = [slice(h * HALF // GROUP, (h + 1) * HALF // GROUP) for h in range(2)]
    blocks = [slice(b * P, (b + 1) * P) for b in range(S // P)]
    all_blocks, first_blocks, second_blocks = range(S // P), (0, 1), (2, 3)

    with ExitStack() as ctx:
        keep = ctx.enter_context(tc.tile_pool(name="keep", bufs=1))
        shared = ctx.enter_context(tc.tile_pool(name="shared", bufs=1))
        psum = ctx.enter_context(tc.psum_pool(name="psum", bufs=1))

        def bank(number):
            return psum.tile([P, S], F32, name="bank_%d" % number)

        offs_sb = keep.tile([P, S // GROUP], U16, name="offs_sb")
        west_sb = keep.tile([P, S // GROUP], U16, name="west_sb")
        east_sb = keep.tile([P, S // GROUP], U16, name="east_sb")
        word_table = keep.tile([P, T], U32, name="word_table", align_bytes=64)
        scale_table = shared.tile([P, T], U8, name="scale_table", offset=3072, align_bytes=64)
        w1_raw = keep.tile([P, PACK, H], F32, name="w1_raw", tag="w1_then_rec", align_bytes=64)
        gain = keep.tile([P, PACK], F32, name="gain")

        nc.gpsimd.memset(scale_table[:].bitcast(I32), 0)
        nc.scalar.dma_start(gain[:], gn.rearrange("(p t) o -> p (t o)", t=PACK))
        w1_rows = w1.rearrange("(p j) c -> p j c", j=PACK)
        nc.sync.dma_start(w1_raw[:, 0:2, :], w1_rows[:, 0:2, :])
        nc.sync.dma_start(offs_sb[:], offs)
        nc.sync.dma_start(scale_table[0:P:8, :].bitcast(I32), x_scales[0].bitcast(I32))
        nc.sync.dma_start(w1_raw[:, 2:4, :], w1_rows[:, 2:4, :])
        nc.sync.dma_start(word_table[:].bitcast(I32), x_words[0].rearrange("p n t -> p (n t)").bitcast(I32))
        picked_scale = keep.tile([P, S], U8, name="picked_scale", align_bytes=64)
        nc.vector.tensor_copy(picked_scale[:], scale_table[:].indirect(offs_sb[:]))
        x_scale = keep.tile([P, S], U8, name="x_scale", align_bytes=64)
        nc.vector.memset(x_scale[:].bitcast(I32), 0)
        for r in range(4):
            nc.sync.dma_start(x_scale[r:P:QUADRANT, :].bitcast(I32), picked_scale[8 * r : P : QUADRANT, :].bitcast(I32))
        w2_rows = w2.rearrange("(p j) c -> p j c", j=PACK)
        w2_raw = [shared.tile([P, PACK, HALF], F32, name="w2_raw_%d" % h, offset=4096 * h, align_bytes=64) for h in range(2)]
        nc.sync.dma_start(w2_raw[0][:], w2_rows[:, :, halves[0]])
        nc.sync.dma_start(west_sb[:], west)
        nc.sync.dma_start(east_sb[:], east)
        nc.sync.dma_start(w2_raw[1][:], w2_rows[:, :, halves[1]])

        ident = keep.tile([P, P], F32, name="ident", align_bytes=64)
        make_identity(nc, ident[:])

        def transpose_into(dst, src, start, stop):
            nc.tensor.matmul(dst, lhsT=src, rhs=ident[:], start=start, stop=stop, is_transpose=True)

        gain_bank = bank(GAIN_BANK)
        for t in range(PACK):
            transpose_into(gain_bank[:, blocks[t]], gain[:, t : t + 1].to_broadcast([P, P]), True, True)
        window_0 = keep.tile([P, 2 * S], F32, name="window_0", tag="window_0", align_bytes=64)
        factor = window_0[:, S : 2 * S].rearrange("q (u p e) -> q u p e", u=2, e=2)
        nc.scalar.activation(factor, gain_bank[:].rearrange("q (u e p) -> q u p e", u=2, e=2), ACT.Copy, scale=-1.0)

        w1_cols = w1_raw[:].rearrange("p j (m t) -> p m j t", t=PACK)
        w1_grouped, w1_codes, w1_scale = [], [], []
        for pair, interleave in enumerate((nc.vector.tensor_copy, nc.scalar.copy)):
            w1_grouped.append(keep.tile([P, 2, P, PACK], BF16, name="w1_grouped_%d" % pair, tag="w1_grouped_%d" % pair, align_bytes=64))
            for rows in ((slice(0, 4),), (slice(0, 2), slice(2, 4)))[pair]:
                interleave(w1_grouped[pair][:].rearrange("p e m j -> p m j e")[:, :, rows, :], w1_cols[:, :, rows, 2 * pair : 2 * pair + 2])

        def quantise_w1(pair, tag):
            w1_codes.append(keep.tile([P, 2 * P], U32, name="w1_codes_%d" % pair, tag=tag, align_bytes=64))
            w1_scale.append(keep.tile([P, 2 * P], U8, name="w1_scale_%d" % pair, align_bytes=64))
            nc.vector.quantize_mx(out=w1_codes[pair][:].bitcast(FP8X4), scales=w1_scale[pair][:],
                                  in_=w1_grouped[pair][:].rearrange("p e m j -> p (e m j)"))

        quantise_w1(0, "w1_codes_0")
        quantise_w1(1, "w1_codes_1")
        x_codes = keep.tile([P, S], U32, name="x_codes", align_bytes=64)
        for h in range(2):
            nc.vector.tensor_copy(x_codes[:, halves[h]], word_table[:].indirect(offs_sb[:, half_entries[h]]))

        rec_sb = keep.tile([P, PACK, S], F32, name="rec_sb", tag="w1_then_rec", align_bytes=64)
        rec_rows = rec.rearrange("(p t) s -> p t s", t=PACK)
        for e in range(2):
            nc.sync.dma_start(rec_sb[:, e:PACK:2, :], rec_rows[:, e:PACK:2, :])

        signed_y, square = [], []
        window_2 = keep.tile([P, 2 * S], F32, name="window_2", tag="window_2", align_bytes=64)
        for t in range(PACK):
            signed_y.append(keep.tile([P, S], F32, name="signed_y_%d" % t, align_bytes=64) if t % 2 else (window_0, window_2)[t // 2][:, 0:S])
            square.append(keep.tile([P, S], F32, name="square_%d" % t, align_bytes=64) if t < 3 else window_2[:, S : 2 * S])

        def first_product(t, cols, number):
            acc = bank(number)
            nc.tensor.matmul_mx(out=acc[:, cols], lhsT=w1_codes[t // 2][:, blocks[t % 2]].bitcast(FP8X4), lhsT_scale=w1_scale[t // 2][:, blocks[t % 2]],
                                rhs=x_codes[:, cols].bitcast(FP8X4), rhs_scale=x_scale[:, cols], start=True, stop=True)
            nc.scalar.activation(signed_y[t][:, cols], acc[:, cols], ACT.Tanh)

        def make_square(t):
            nc.scalar.activation(square[t][:], signed_y[t][:], ACT.Square, scale=math.sqrt(0.3125))

        first_product(0, halves[0], 1)
        first_product(1, halves[0], 6)
        first_product(0, halves[1], 7)
        first_product(1, halves[1], 2)
        make_square(0)
        first_product(2, slice(0, S), 3)
        make_square(1)
        first_product(3, slice(0, S), 4)
        make_square(2)
        make_square(3)

        w2_grouped, w2_codes, w2_scale = [], [], []

        def quantise_w2(h, tag, pieces):
            w2_codes.append(keep.tile([P, HALF], U32, name="w2_codes_%d" % h, tag=tag, align_bytes=64))
            w2_scale.append(keep.tile([P, HALF], U8, name="w2_scale_%d" % h, align_bytes=64))
            for cols in pieces:
                nc.vector.quantize_mx(out=w2_codes[h][:, cols].bitcast(FP8X4), scales=w2_scale[h][:, cols], in_=w2_grouped[h][:, cols, :].rearrange("p c j -> p (c j)"))

        w2_grouped.append(keep.tile([P, HALF, PACK], BF16, name="w2_grouped_0", align_bytes=64))

        def cast_w2(h, cols, move):
            move(w2_grouped[h][:, cols, :], w2_raw[h][:, :, cols].rearrange("p j c -> p c j"))

        for m in range(2):
            cast_w2(0, blocks[m], nc.vector.tensor_copy)
        quantise_w2(0, "w2_codes_0", blocks[0:2])

        cubic, near = [], {}

        def vector_neighbours(t, tag):
            near[t] = keep.tile([P, 2, S], F32, name="near_%d" % t, tag=tag, align_bytes=64)
            for side, cells in ((0, slice(0, S)), (1, halves[0]), (1, halves[1])):
                window = window_2[:].indirect((west_sb, east_sb)[side][:, cells.start // GROUP : cells.stop // GROUP])
                nc.vector.tensor_scalar(near[t][:, side, cells], window, -0.25, 0.0, ALU.mult, ALU.add)

        near[0] = keep.tile([P, 2, S], F32, name="near_0", align_bytes=64)
        for side, places in enumerate((west_sb, east_sb)):
            nc.vector.tensor_scalar(near[0][:, side, :], window_0[:].indirect(places[:]), -0.25, 0.0, ALU.mult, ALU.add)
        for t in range(PACK):
            if t in SCALAR_PLANES:
                near[t] = keep.tile([P, 2, S], F32, name="near_%d" % t, align_bytes=64)
            cubic.append(keep.tile([P, S], F32, name="cubic_%d" % t, align_bytes=64))
            nc.vector.scalar_tensor_tensor(cubic[t][:], square[t][:], 1.0, signed_y[t][:], ALU.subtract, ALU.mult)
        vector_neighbours(2, "near_2")
        w2_grouped.append(keep.tile([P, HALF, PACK], BF16, name="w2_grouped_1", tag="window_2", align_bytes=64))
        nc.gpsimd.tensor_scalar(w2_grouped[1][:, 0:SPLIT, :], w2_raw[1][:, :, 0:SPLIT].rearrange("p j c -> p c j"), 1.0, 0.0, ALU.mult, ALU.add)
        for t, cells in ((1, halves[0]), (3, halves[0]), (1, halves[1]), (3, blocks[2]), (3, blocks[3])):
            for side, places in enumerate((west_sb, east_sb)):
                entries = slice(cells.start // GROUP, cells.stop // GROUP)
                nc.scalar.activation(near[t][:, side, cells], signed_y[t][:].indirect(places[:, entries]), ACT.Copy, scale=-0.25)


        cast_w2(1, slice(SPLIT, HALF), nc.scalar.copy)

        sums = [bank(number) for number in (5, 6, 7, 0, 1)]

        def add_term(t, term, where, start=False, stop=False):
            for b in where:
                if b < 3:
                    transpose_into(sums[b][:, blocks[2 * (t % 2) + t // 2]], term[:, blocks[b]], start and t == 0, stop)
                else:
                    transpose_into(sums[3 + t // 2][:, blocks[t % 2]], term[:, blocks[b]], start, stop)

        back = {}
        z_codes = keep.tile([P, S], U32, name="z_codes", align_bytes=64)
        z_scale = keep.tile([P, S], U8, name="z_scale", align_bytes=64)

        def leave(b, number):
            back[b] = bank(number)
            z_turned = keep.tile([P, 2, P, 2], BF16, name="z_turned_%d" % b, tag="z_turned_%d" % b, align_bytes=64)
            nc.vector.tensor_tensor(z_turned[:].rearrange("q u p e -> q (u p) e"), sums[b][:].rearrange("q (e c) -> q c e", e=2),
                                    window_0[:, S : 2 * S].rearrange("q (c e) -> q c e", e=2), ALU.mult)
            for u in range(2):
                transpose_into(back[b][:, blocks[u]], z_turned[:, u].rearrange("q p e -> q (p e)").bitcast(F32), True, True)

        def leave_last(u, tag):
            z_turned = keep.tile([P, P, 2], BF16, name="z_last_%d" % u, tag=tag, align_bytes=64)
            nc.vector.tensor_tensor(z_turned[:], sums[3 + u][:, halves[0]].rearrange("q (e p) -> q p e", e=2), factor[:, u], ALU.mult)
            transpose_into(back[3][:, blocks[u]], z_turned[:].rearrange("q p e -> q (p e)").bitcast(F32), True, True)

        def quantise_z(b, unpack):
            z_grouped = keep.tile([P, P * PACK], BF16, name="z_grouped_%d" % b, tag="z_grouped_%d" % b, align_bytes=64)
            unpack(z_grouped[:].bitcast(F32).rearrange("p (c u) -> p c u", u=2), back[b][:, 0 : 2 * P].rearrange("p (u c) -> p c u", u=2))
            nc.vector.quantize_mx(out=z_codes[:, blocks[b]].bitcast(FP8X4), scales=z_scale[:, blocks[b]], in_=z_grouped[:])

        for t in VECTOR_PLANES:
            add_term(t, rec_sb[:, t, :], all_blocks, start=True)
        add_term(0, near[0][:, 0, :], all_blocks)
        for t in SCALAR_PLANES:
            add_term(t, rec_sb[:, t, :], all_blocks)
        add_term(0, near[0][:, 1, :], all_blocks)
        for t in range(2):
            add_term(t, cubic[t][:], all_blocks)
        for side in range(2):
            add_term(1, near[1][:, side, :], first_blocks)
            add_term(2 + side, cubic[2 + side][:], all_blocks)
        for side in range(2):
            for t in (3, 2):
                add_term(t, near[t][:, side, :], first_blocks, stop=(t, side) == (2, 1))
        for side in range(2):
            add_term(1, near[1][:, side, :], (2,))
            add_term(1, near[1][:, side, :], (3,), stop=side == 1)
            add_term(2, near[2][:, side, :], second_blocks)
        for side in range(2):
            add_term(3, near[3][:, side, :], (2,), stop=side == 1)
        leave(0, 2)
        for side in range(2):
            add_term(3, near[3][:, side, :], (3,), stop=side == 1)
        leave(1, 3)
        leave(2, 4)
        back[3] = bank(5)
        leave_last(0, "z_last_0")
        quantise_z(0, nc.scalar.copy)
        leave_last(1, "z_turned_1")
        quantise_z(1, nc.scalar.copy)
        quantise_w2(1, "window_0", halves[0:1])
        quantise_z(2, nc.scalar.copy)
        quantise_z(3, nc.vector.tensor_copy)

        out_rows = out.rearrange("(m p) c -> p m c", p=P)

        def multiply(cells, tiles, number):
            acc = bank(number)
            width = cells.stop - cells.start
            for i, m in enumerate(tiles):
                nc.tensor.matmul_mx(out=acc[:, i * width : (i + 1) * width], lhsT=w2_codes[m // 2][:, blocks[m % 2]].bitcast(FP8X4),
                                    lhsT_scale=w2_scale[m // 2][:, blocks[m % 2]],
                                    rhs=z_codes[:, cells].bitcast(FP8X4), rhs_scale=z_scale[:, cells], start=True, stop=True)
            return acc[:, 0 : len(tiles) * width].rearrange("p (m c) -> p m c", c=width)

        def send(cells, tiles, number, empty, queue):
            result = keep.tile([P, len(tiles), cells.stop - cells.start], F32, name="result_%d_%d" % (cells.start, tiles[0]), align_bytes=64)
            empty(result[:], multiply(cells, tiles, number))
            queue.dma_start(out_rows[:, tiles[0] : tiles[-1] + 1, cells], result[:])

        send(blocks[0], (0, 1), 6, nc.scalar.copy, nc.sync)
        send(blocks[1], (0, 1), 7, nc.scalar.copy, nc.sync)
        send(halves[0], (2,), 0, nc.scalar.copy, nc.sync)
        send(halves[0], (3,), 2, nc.scalar.copy, nc.sync)
        late = [keep.tile([P, 2, HALF], F32, name="late_%d" % pair, align_bytes=64) for pair in range(2)]
        for pair, number in enumerate((1, 3)):
            nc.vector.tensor_copy(late[pair][:, :, blocks[0]], multiply(blocks[2], (2 * pair, 2 * pair + 1), number))
        for m, (number, empty, queue) in enumerate(((4, nc.scalar.copy, nc.sync), (5, nc.vector.tensor_copy, nc.sync),
                                                    (6, nc.scalar.copy, nc.scalar), (7, nc.vector.tensor_copy, nc.sync))):
            row = late[m // 2][:, m % 2 : m % 2 + 1, :]
            empty(row[:, :, blocks[1]], multiply(blocks[3], (m,), number))
            queue.dma_start(out_rows[:, m : m + 1, halves[1]], row)
